import numpy as np, ml_dtypes
CORES = [40,41,42,43,44,45,46,47]
N = 8
BF = ml_dtypes.bfloat16
S, M, CAP, L = 512, 512, 112, 6
F = 16 // N
def tries(rng, same=False, few=False):
    kid = np.zeros((N, 8, M, 16), np.int32); words = {}; deep = {}
    tid = (rng.integers(1, 65536, (N, 8, M)) * (rng.random((N, 8, M)) < (0.0625 if few else 0.5))).astype(np.int32)
    for q in range(N):
        for g in range(8):
            no = [0, 1] + (2 + rng.permutation(M - 2)).tolist(); pl = rng.random(M).tolist(); cl = rng.integers(0, 16, M).tolist()
            k = kid[q, g]; w = {1: []}; up = []; m = 2; deep[q, g] = []
            for c in (q * F + rng.permutation(F)).tolist()[:1 if few else F]:
                p = 1
                for d in range(L):
                    e = c if d == 0 or same else cl[m]
                    k[no[p], e] = no[m]; w[m] = w[p] + [e]
                    if d < L - 1: up.append(m)
                    p = m; m += 1
                tid[q, g, no[p]] = rng.integers(1, 65536); deep[q, g].append(w[p])
            for m in range(m, M):
                p = up[int(pl[m] * len(up))]; e = cl[m]
                if k[no[p], e]: continue
                k[no[p], e] = no[m]; w[m] = w[p] + [e]
                if len(w[m]) < L: up.append(m)
            words[q, g] = [v for v in w.values() if v]
    tid[:, :, 0] = 0
    return kid.reshape(N, 8, 16 * M), tid, words, deep
def strings(rng, words):
    s = np.zeros((8, N * S), np.int64)
    for g in range(8):
        qs = rng.integers(0, N, N * S).tolist(); ms = rng.random(N * S).tolist(); a = []; i = 0
        while len(a) < N * S:
            v = words[qs[i], g]; a += v[int(ms[i] * len(v))]; i += 1
        s[g] = a[:N * S]
    return np.where(rng.random(s.shape) < 0.1, rng.integers(0, 16, s.shape), s)
def plant(rng, s, deep):
    keep = np.zeros(s.shape, bool)
    for r in range(N):
        for g in range(8):
            v = deep[int(rng.integers(0, N)), g]; j = (r * S + S - 1 - g % (L - 1) + np.arange(L)) % (N * S)
            s[g, j] = v[int(rng.integers(0, len(v)))]; keep[g, j] = True
    return keep
def fit(rng, s, keep, full=False):
    s = s.reshape(8, N, S).transpose(1, 0, 2).astype(np.int32); keep = keep.reshape(8, N, S).transpose(1, 0, 2)
    a, b = int(rng.integers(0, N)), int(rng.integers(0, 8))
    for r in range(N):
        for g in range(8):
            e = s[r, g]; own = e // F; have = np.bincount(own, minlength=N); low = np.bincount(own[keep[r, g]], minlength=N)
            o = rng.permutation(N); i = np.flatnonzero((o == a) if full and g == b else (o != r))[0]; o[[0, i]] = o[[i, 0]]
            want = low.copy() if full else np.minimum(have, CAP)
            if full or (r, g) == (a, b): want[o[0]] = CAP
            for q in np.roll(o, -1): want[q] = min(max(int(want[q]) + S - int(np.sum(want)), int(low[q])), CAP)
            sur = np.concatenate([rng.permutation(np.flatnonzero((own == q) & ~keep[r, g]))[:max(int(have[q] - want[q]), 0)] for q in range(N)])
            need = np.repeat(np.arange(N), np.maximum(want - have, 0))
            e[sur] = need * F + rng.integers(0, F, len(need))
    return np.ascontiguousarray(s)
def setup_inputs(rng):
    kid, tid, words, deep = tries(rng); s = strings(rng, words); keep = plant(rng, s, deep)
    return {"lett": fit(rng, s, keep), "kid": kid, "tid": tid}
def setup_inputs_full(rng):
    kid, tid, words, deep = tries(rng); s = strings(rng, words)
    lett = fit(rng, s, np.zeros(s.shape, bool), True)
    assert np.sum((lett // F)[..., None] == np.arange(N), axis=2).min(axis=0).max() == CAP
    return {"lett": lett, "kid": kid, "tid": tid}
def setup_inputs_runs(rng):
    kid, tid, words, deep = tries(rng, same=True)
    s = np.stack([np.repeat(rng.integers(0, 16, N * S), rng.integers(1, 13, N * S))[:N * S] for g in range(8)]); keep = plant(rng, s, deep)
    return {"lett": fit(rng, s, keep), "kid": kid, "tid": tid}
def setup_inputs_few(rng):
    kid, tid, words, deep = tries(rng, few=True); s = strings(rng, words); keep = plant(rng, s, deep)
    return {"lett": fit(rng, s, keep), "kid": kid, "tid": tid}
def setup_inputs_spread(rng):
    kid = (rng.integers(0, M, (N, 8, M, 16)) * (rng.random((N, 8, M, 16)) > 0.125)).astype(np.int32)
    kid[:, :, 0] = 0; kid[:, :, 1] *= (np.arange(16) // F == np.arange(N)[:, None])[:, None, :]
    tid = (rng.integers(0, 65536, (N, 8, M)) * (rng.random((N, 8, M)) < 0.3)).astype(np.int32); tid[:, :, 0] = 0; tid[:, :, M - 1] = 65535
    s = np.minimum(np.floor(rng.random((8, N * S)) ** 2 * 16), 15).astype(np.int64)
    return {"lett": fit(rng, s, np.zeros(s.shape, bool)), "kid": kid.reshape(N, 8, 16 * M), "tid": tid}
def check_inputs(d):
    bad = []; s, kid, tid = d["lett"], d["kid"], d["tid"]
    if s.min() < 0 or s.max() > 15: bad.append("letters")
    if ((s // F)[..., None] == np.arange(N)).sum(2).max() > CAP: bad.append("slots")
    if kid.min() < 0 or kid.max() >= M: bad.append("children")
    if kid[:, :, :16].any() or tid[:, :, 0].any(): bad.append("node 0")
    if (kid[:, :, 16:32] * (np.arange(16) // F != np.arange(N)[:, None])[:, None, :]).any(): bad.append("roots")
    if tid.min() < 0 or tid.max() > 65535: bad.append("ids")
    return bad
def reference(lett, kid, tid):
    s = np.concatenate(list(lett), axis=1).astype(np.int64)
    own = s // F; g = np.arange(8)[:, None]; node = np.ones(s.shape, np.int64); yl = np.zeros(s.shape, np.int64); yi = np.zeros(s.shape, np.int64)
    for k in range(L):
        node = kid[own, g, 16 * node + np.roll(s, -k, axis=1)].astype(np.int64)
        t = tid[own, g, node]
        yl = np.where(t > 0, k + 1, yl); yi = np.where(t > 0, t, yi)
    yl = np.ascontiguousarray(yl.reshape(8, N, S).transpose(1, 0, 2)); yi = np.ascontiguousarray(yi.reshape(8, N, S).transpose(1, 0, 2))
    return {"ylen": yl.astype(np.float32), "yid": yi.astype(np.float32)}

@@ -1,0 +1,351 @@
+from concourse.bass import DstId, RemoteDMATransfer
+from concourse.mybir import AluOpType as A, ActivationFunctionType as F
+
+N = 8
+SCRATCH = {"rl": ("dram", [8, 128, 2], "int32"), "idl": ("dram", [8, 128, 64], "bfloat16"),
+           "kraw": ("sbuf", [128, 32, 16], "int32"), "kb": ("sbuf", [128, 8, 64], "bfloat16"),
+           "wr": ("sbuf", [128, 4, 128], "bfloat16"), "wi": ("sbuf", [128, 8, 128], "bfloat16")}
+for _d, _names in (("bfloat16", "win4096 idwin4096 pw384 pf16 bs8 idp384 wlb32 halob8 idhi128 idlo128 iom128 ioa128 blk128 "
+                                "shift128 last128 z512 em592 xa256 xb256"),
+                   ("int32", "wl32 halo32 wa32 wb32 wd32 we32 wf32 wg32 wh32 wj32 wq32 tidr128 ta128 tz128 tl128 pgi1 iop1 ri1 "
+                             "wsi1 keyi32 leni32 idi32"),
+                   ("float32", "lp24 pg1 iof16 rr1 ws1 rm16 eq8 dd4 da4 db4 ca1 cb1 lowr1 ea1 eb1 bc1 bk6 "
+                               "zer32 dk128 dz64 dy192 dv128 sca64 scb64 scy192 scv128 scz128 top32 best32 yl32 yi32"),
+                   ("uint16", "lone2 ltwo2 lpre24 lc32 lq32")):
+    for _n in _names.split():
+        _b = _n.rstrip("0123456789")
+        SCRATCH[_b] = ("sbuf", [128, int(_n[len(_b):])], _d)
+for _k in range(1, 7):
+    if _k > 2:
+        SCRATCH["l%d" % _k] = ("sbuf", [128, 32], "uint16")
+    SCRATCH["y%d" % _k] = ("sbuf", [128, 512], "bfloat16")
+for _k in range(6):
+    SCRATCH["p%d" % _k] = ("psum", [128, 512], "float32")
+SEMAPHORES = ["cv", "cs", "ct", "cg", "dl", "dr", "dt", "dhi", "dlo", "drr", "didw", "dyl", "dyi"] + \
+             [a + b for a in ("r", "id", "x", "p", "n", "k") for b in ("_in", "_out")] + ["dk%d" % k for k in range(4)]
+
+
+def rank_program(g, core, T, topo):
+    me = T.rank_of(core)
+    if me is None:
+        return
+    q = {"v": g.vector, "s": g.scalar, "t": g.tensor, "g": g, "y": g.sync}
+    total, seen = {}, {k: {} for k in q}
+
+    def wait(k, *toks):
+        for tok in toks:
+            if tok is not None and seen[k].get(tok[0], 0) < tok[1]:
+                q[k].wait_ge(T.sem[tok[0]], tok[1])
+                seen[k][tok[0]] = tok[1]
+
+    def done(sem, inst, n=1):
+        inst.then_inc(T.sem[sem], n)
+        total[sem] = total.get(sem, 0) + n
+        return (sem, total[sem])
+
+    def V(inst): return done("cv", inst)
+    def S(inst): return done("cs", inst)
+    def P(inst): return done("ct", inst)
+    def G(inst): return done("cg", inst)
+    v, s, t, sy = g.vector, g.scalar, g.tensor, g.sync
+    H, NB = N // 2, 48
+    peers = [T.cores[(me + d) % N] for d in range(1, N)]
+    pos = [2 * (j % H) + j // H for j in range(N)]
+    at, partner = me % H, T.cores[(me + H) % N]
+    near = [T.cores[me - at + (at + d) % H] for d in range(1, H)]
+    wb0, pb0 = 512 * pos[me], NB * pos[me]
+
+    def dst(c):
+        a = topo.addr(c)
+        return DstId(rid=a[0], pnc=a[1])
+
+    def send(src, name, to):
+        mask = topo.mask(core, to[0])
+        for c in to:
+            mask = mask & topo.mask(core, c)
+        ne = bin(mask).count("1")
+        g.remote_dma_fused([RemoteDMATransfer(dst_ids=[dst(c) for c in to], dma_engine_mask=mask,
+                                              remote_sem=T.sem[name + "_in"], srcs=[src], dsts=[src for c in to])],
+                           local_sem=T.sem[name + "_out"])
+        total[name + "_out"] = ne
+        total[name + "_in"] = ne * len(to)
+        return (name + "_in", ne * len(to))
+
+    r_own = done("dr", sy.dma_start(T.rl[me], T.lett[:, 0:32]), 16)
+    tid_ld = done("dt", s.dma_start(T.tidr[0:32, :], T.tid[:]), 16)
+    kid_ld = []
+    for j in range(4):
+        a, gl = j // 2, j % 2
+        kid_ld.append(done("dk%d" % j, (sy, s)[gl].dma_start(T.kraw[:, 16 * gl + 8 * a:16 * gl + 8 * a + 8, :],
+                                                             T.kid[gl::2, 4096 * a:4096 * a + 4096]), 16))
+    lett_ld = done("dl", sy.dma_start(T.wl[:], T.lett[:]), 16)
+
+    ip = G(g.iota(T.iop[:], [[0, 1]], 0, 1))
+    io = G(g.iota(T.iom[:], [[16, 8], [0, 16]], 0, 0, allow_small_or_imprecise_dtypes=True))
+    iof = G(g.iota(T.iof[:], [[1, 16]], 0, 0, allow_small_or_imprecise_dtypes=True))
+    bs = G(g.iota(T.bs[:], [[512, 8]], 256, 0, allow_small_or_imprecise_dtypes=True))
+    idz = V(v.memset(T.idwin[:, 0:512], 0.0))
+    hz = V(v.memset(T.halo[:], 0))
+    V(v.memset(T.pw[:, pb0 + 32:pb0 + NB], 0.0))
+    wait("v", ip)
+    V(v.tensor_scalar(T.pgi[:], T.iop[:], 112, None, A.bitwise_and))
+    k0 = V(v.tensor_scalar(T.ri[:], T.iop[:], 15, None, A.bitwise_and))
+    V(v.memset(T.eq[:], 1.0))
+    wait("v", k0)
+    kp = V(v.tensor_copy(T.pg[:], T.pgi[:]))
+    k1 = V(v.tensor_copy(T.rr[:], T.ri[:]))
+    k2 = V(v.tensor_scalar(T.wsi[:], T.ri[:], 2, None, A.arith_shift_right))
+    wait("v", io, kp)
+    bl = V(v.tensor_scalar(T.blk[:], T.iom[:], T.pg[:, 0:1], None, A.is_equal))
+    wait("v", k1, iof)
+    rm = V(v.tensor_scalar(T.rm[:], T.iof[:], T.rr[:, 0:1], None, A.is_equal))
+
+    wait("v", tid_ld)
+    V(v.tensor_scalar(T.ta[0:32, :], T.tidr[0:32, :], 65280, None, A.bitwise_and))
+    a3 = V(v.tensor_scalar(T.tz[0:32, :], T.tidr[0:32, :], 0, -524288, A.is_equal, A.mult))
+    a4 = V(v.tensor_scalar(T.tl[0:32, :], T.tidr[0:32, :], 255, None, A.bitwise_and))
+    wait("v", a3)
+    hi = V(v.tensor_tensor(T.idhi[0:32, :], T.ta[0:32, :], T.tz[0:32, :], A.add))
+    wait("v", a4)
+    lo = V(v.tensor_copy(T.idlo[0:32, :], T.tl[0:32, :]))
+    wait("y", hi)
+    hi_st = done("dhi", sy.dma_start(T.idl[me, 0:64, :], T.idhi[0:32, :]), 16)
+    wait("y", lo)
+    lo_st = done("dlo", sy.dma_start(T.idl[me, 64:128, :], T.idlo[0:32, :]), 16)
+
+    wait("g", r_own)
+    r_in = send(T.rl[me], "r", [T.cores[(me - 1) % N]])
+    io4 = G(g.iota(T.ioa[:], [[16, 8], [0, 4], [1, 4]], 0, 0, allow_small_or_imprecise_dtypes=True))
+    wait("g", hi_st, lo_st)
+    id_in = send(T.idl[me], "id", peers)
+
+    wait("s", idz)
+    S(s.activation(T.zer[:], T.idwin[:, 0:32], F.Copy))
+    for n in (512, 1024, 2048):
+        idz = S(s.activation(T.idwin[:, n:2 * n], T.idwin[:, 0:n], F.Copy))
+        wait("s", idz)
+
+    for j in range(4):
+        a, gl = j // 2, j % 2
+        wait("v", kid_ld[j])
+        kc = V(v.tensor_scalar(T.kb[:, :, 32 * a + 16 * gl:32 * a + 16 * gl + 16],
+                               T.kraw[:, 16 * gl + 8 * a:16 * gl + 8 * a + 8, :], 256, None, A.subtract))
+        if j == 1:
+            k3 = V(v.tensor_scalar(T.bc[:], T.rr[:], 2.0, 65536.0, A.is_equal, A.mult))
+            wait("v", k2)
+            k4 = V(v.tensor_copy(T.ws[:], T.wsi[:]))
+    wait("v", kc)
+    for m in (1, 0, 2, 3, 4, 5, 6, 7):
+        ev = V(v.transpose(T.win[:, wb0 + m:wb0 + 512:8], T.kb[:, m, :]))
+        if m == 1:
+            root = ev
+        if m == 6:
+            wait("v", root)
+            l1 = V(v.tensor_scalar(T.lone[:, 0:1], T.win[:, wb0 + 1:wb0 + 2], 256, None, A.add))
+    wait("g", ev)
+    x_in = send(T.win[:, wb0:wb0 + 512], "x", [partner])
+
+    wait("v", ev, l1)
+    g1 = V(v.tensor_copy(T.pf[:], T.win[:, wb0:wb0 + 512].indirect(T.lone[:, 0:1])))
+    V(v.tensor_copy(T.pw[:, pb0 + 34:pb0 + 35], T.win[:, wb0 + 1:wb0 + 2]))
+    wait("v", g1)
+    l2 = V(v.tensor_scalar(T.ltwo[:], T.pf[:, 2 * me:2 * me + 2], 256, None, A.add))
+    V(v.tensor_copy(T.pw[:, pb0 + 32:pb0 + 34], T.pf[:, 2 * me:2 * me + 2]))
+    wait("v", l2)
+    p3 = V(v.tensor_copy(T.pw[:, pb0:pb0 + 32], T.win[:, wb0:wb0 + 512].indirect(T.ltwo[:])))
+    wait("v", k4, lett_ld)
+    wb = V(v.tensor_copy(T.wlb[:], T.wl[:]))
+    wait("g", p3)
+    p_in = send(T.pw[:, pb0:pb0 + NB], "p", [partner])
+    wait("g", bl)
+    G(g.affine_select(T.shift[:], T.blk[:], [[1, 128]], A.is_equal, 0.0, 1, -1))
+    sh = G(g.affine_select(T.last[:], T.blk[:], [[1, 128]], A.is_equal, 0.0, -15, -1))
+    wait("g", p_in)
+    n_in = send(T.pw[:, 2 * NB * at:2 * NB * at + 2 * NB], "n", near)
+    wait("g", x_in)
+    k_in = send(T.win[:, 1024 * at:1024 * at + 1024], "k", near)
+    for i in range(8):
+        wi = G(g.affine_select(T.wi[:, i, :], T.blk[:], [[0, 16], [1, 8]], A.is_equal, 0.0, -i, 0))
+    wait("y", r_in, hz)
+    rr_ld = done("drr", sy.dma_start(T.halo[0:128:16, :], T.rl[(me + 1) % N]), 16)
+
+    wait("s", wb, rm)
+    for r in range(16):
+        zs = S(s.activation(T.z[:, r::16], T.wlb[:], F.Copy, scale=T.rm[:, r:r + 1]))
+    c1 = V(v.tensor_scalar(T.eq[:, 0:4], T.iof[:, 0:4], T.ws[:, 0:1], None, A.is_equal))
+    V(v.tensor_scalar(T.wa[:], T.wl[:], 6, None, A.bitwise_and))
+    c2 = V(v.tensor_scalar(T.wb[:], T.wl[:], 3, None, A.arith_shift_right))
+    wait("v", c1)
+    c3 = V(v.tensor_tensor(T.dd[:], T.eq[:, 0:4], T.eq[:, 1:5], A.subtract))
+    low = V(v.tensor_scalar(T.lowr[:], T.ws[:], 2.0, None, A.is_lt))
+    c5 = V(v.tensor_scalar(T.wd[:], T.wl[:], 1, None, A.bitwise_and))
+    wait("v", c2)
+    c2 = V(v.tensor_tensor(T.wq[:], T.wa[:], T.wb[:], A.add))
+    wait("v", rr_ld)
+    hb = V(v.tensor_copy(T.halob[:], T.halo[:, 0:8]))
+    wait("v", c5)
+    c5 = V(v.tensor_scalar(T.we[:], T.wd[:], 16, None, A.mult))
+    wait("v", c2)
+    c7 = V(v.tensor_scalar(T.wf[:], T.wq[:], NB, None, A.mult))
+    wait("v", c5)
+    V(v.tensor_tensor(T.wg[:, 0:31], T.we[:, 0:31], T.wl[:, 1:32], A.add))
+    wait("v", c7)
+    c7 = V(v.tensor_tensor(T.wj[:], T.wf[:], T.wl[:], A.add))
+    wait("t", wb, hb, bl, sh)
+    P(t.matmul(T.p3[:, 0:1], T.shift[:], T.wlb[:, 0:1], True, False))
+    cn = P(t.matmul(T.p3[:, 0:1], T.last[:], T.halob[:, 0:1], False, True))
+    P(t.matmul(T.p5[:, 0:5], T.blk[:], T.halob[:, 0:5], True, True))
+    wait("t", zs)
+    el = P(t.matmul(T.p4[:], T.blk[:], T.z[:], True, True))
+    wait("v", io4)
+    for i in range(4):
+        V(v.tensor_scalar(T.wr[:, i, :], T.ioa[:], float(-i), T.pg[:, 0:1], A.add, A.is_equal))
+    wait("v", c7)
+    V(v.tensor_copy(T.lc[:], T.wj[:]))
+    wait("v", cn)
+    c6 = V(v.tensor_scalar(T.wg[:, 31:32], T.we[:, 31:32], T.p3[:, 0:1], None, A.add))
+    wait("v", el)
+    em = V(v.tensor_scalar(T.em[:, 512:591], T.p4[:, 1:80], T.rr[:, 0:1], None, A.is_equal))
+    wait("v", c6)
+    c6 = V(v.tensor_tensor(T.wh[:], T.wf[:], T.wg[:], A.add))
+    V(v.tensor_scalar(T.em[:, 0:512], T.p4[:], T.rr[:, 0:1], None, A.is_equal))
+    wait("v", em, c6)
+    lq = V(v.tensor_copy(T.lq[:], T.wh[:]))
+    em = V(v.tensor_scalar(T.em[:, 527:592:16], T.p5[:, 0:5], T.rr[:, 0:1], None, A.is_equal))
+
+    wait("s", c3, low, k3, iof)
+    S(s.activation(T.da[:], T.dd[:], F.Identity, scale=16384.0))
+    c4 = S(s.activation(T.ca[:], T.dd[:, 3:4], F.Identity, bias=-7936.0, scale=16384.0))
+    S(s.activation(T.db[:], T.dd[:], F.Identity, scale=1048576.0))
+    S(s.activation(T.cb[:], T.dd[:, 3:4], F.Identity, bias=-2097152.0, scale=1048576.0))
+    S(s.activation(T.ea[:], T.lowr[:], F.Identity, bias=-1048576.0, scale=2097152.0))
+    c8 = S(s.activation(T.eb[:], T.lowr[:], F.Identity, bias=-2097152.0, scale=-1048576.0))
+    S(s.activation(T.bk[:], T.iof[:, 1:7], F.Copy, scale=T.bc[:, 0:1]))
+    wait("s", c4)
+    for w in range(3):
+        c9 = S(s.activation(T.dk[:, w::4], T.zer[:], F.Identity, bias=T.da[:, w:w + 1]))
+
+    wait("y", id_in, hi_st, lo_st, idz)
+    for j in range(N):
+        b = 512 * pos[j]
+        done("didw", sy.dma_start(T.idwin[0:128:16, b:b + 512], T.idl[j, 0:64, :]), 16)
+        done("didw", sy.dma_start(T.idwin[1:128:16, b:b + 512], T.idl[j, 64:128, :]), 16)
+    idw = ("didw", total["didw"])
+
+    wait("s", c8)
+    for w in range(4):
+        S(s.activation(T.dz[:, w::4], T.zer[:, 0:16], F.Identity, bias=T.db[:, w:w + 1] if w < 3 else T.cb[:, 0:1]))
+    for d, n in ((T.dy, 3), (T.dv, 2)):
+        for w in range(2 * n):
+            if w in (n - 1, 2 * n - 1):
+                cy = S(s.activation(d[:, w::2 * n], T.zer[:], F.Identity, bias=(T.ea if w == n - 1 else T.eb)[:, 0:1]))
+            else:
+                cy = S(s.activation(d[:, w::2 * n], T.zer[:], F.Copy))
+    X = [T.xa, T.xb]
+    SC = [T.sca, T.scb]
+
+    def kid_sum(h, tok):
+        wait("t", tok)
+        for i in range(4):
+            r = P(t.matmul(T["p%d" % h][:, 0:64], T.wr[:, i, :], X[h][:, i::4], i == 0, i == 3))
+        return r
+
+    yt, ys, lt, sc, xt, ks = {}, {}, {}, {}, {}, {}
+
+    def id_sum(k):
+        wait("t", yt[k, 0], yt[k, 1], wi)
+        out = T.p2[:, k - 1:192:3] if k < 4 else T.p3[:, k - 4:128:2]
+        for i in range(8):
+            ys[k] = P(t.matmul(out, T.wi[:, i, :], T["y%d" % k][:, i::8], i == 0, i == 7))
+
+    sums = {(3, 1): [1], (4, 1): [2, 3], (5, 1): [4], (6, 0): [5]}
+
+    def scan(k, h):
+        wait("v", ks[h], dcon, c9)
+        sc[h] = V(v.tensor_tensor_scan(SC[h][:], T["p%d" % h][:, 0:64], T.dk[:, 64 * h:64 * h + 64], -8192.0, A.max, A.add))
+
+    def node_list(k, h):
+        wait("v", sc[h])
+        lt[h] = V(v.tensor_scalar(T["l%d" % k][:, 16 * h:16 * h + 16], SC[h][:, 3::4], 8192.0, None, A.add))
+
+    def gathers(k, h):
+        off = T["l%d" % k][:, 16 * h:16 * h + 16]
+        y, bias = T["y%d" % k][:, 256 * h:256 * h + 256], T.bk[:, k - 1:k]
+        if k < 6:
+            wait("v", lt[h], x_in, k_in, ev)
+            xt[h] = V(v.tensor_tensor(X[h][:], T.win[:].indirect(off), T.em[:, 16 * (k + 16 * h):16 * (k + 16 * h) + 256],
+                                      A.mult))
+            ks[h] = kid_sum(h, xt[h])
+        if k < 6 or h == 0:
+            wait("s", lt[h], idw)
+            yt[k, h] = S(s.activation(y, T.idwin[:].indirect(off), F.Identity, bias=bias))
+        else:
+            wait("v", lt[h], idw)
+            yt[k, h] = V(v.tensor_scalar(y, T.idwin[:].indirect(off), bias, None, A.add))
+        for a in sums.get((k, h), []):
+            id_sum(a)
+
+    for h in range(2):
+        wait("v", em, lq, p3, p_in, n_in)
+        xt[h] = V(v.tensor_tensor(X[h][:], T.pw[:].indirect(T.lq[:, 16 * h:16 * h + 16]),
+                                  T.em[:, 16 * (2 + 16 * h):16 * (2 + 16 * h) + 256], A.mult))
+        ks[h] = kid_sum(h, xt[h])
+        if h == 0:
+            wait("v", bs)
+            for i in range(3):
+                b = V(v.tensor_tensor(T.lp[:, i::3], T.pw[:, 32 + i::NB], T.bs[:], A.add))
+            wait("v", c4)
+            dcon = V(v.tensor_scalar(T.dk[:, 3::4], T.wq[:], 512.0, T.ca[:, 0:1], A.mult, A.add))
+            wait("v", b)
+            lp = V(v.tensor_copy(T.lpre[:], T.lp[:]))
+    wait("s", lp, idw, cy)
+    idp = S(s.activation(T.idp[:], T.idwin[:].indirect(T.lpre[:]), F.Copy))
+    wait("s", idp)
+    for h in range(2):
+        yt[1, h] = S(s.activation(T.y1[:, 256 * h:256 * h + 256], T.idp[:, 32:384].indirect(T.lc[:, 16 * h:16 * h + 16]),
+                                  F.Identity, bias=T.bk[:, 0:1]))
+    for h in range(2):
+        yt[2, h] = S(s.activation(T.y2[:, 256 * h:256 * h + 256], T.idp[:].indirect(T.lq[:, 16 * h:16 * h + 16]),
+                                  F.Identity, bias=T.bk[:, 1:2]))
+
+    for k in range(3, 7):
+        scan(k, 0)
+        if k == 6:
+            wait("v", ys[3], cy)
+            b = V(v.tensor_tensor_scan(T.scy[:], T.p2[:, 0:192], T.dy[:], -2097152.0, A.max, A.add))
+        scan(k, 1)
+        for h in range(2):
+            node_list(k, h)
+        if k == 6:
+            wait("v", b)
+            V(v.tensor_scalar(T.top[:], T.scy[:, 5::6], -2097152.0, None, A.max))
+        for h in range(2):
+            gathers(k, h)
+    for h in range(2):
+        wait("t", yt[6, h])
+        for i in range(4):
+            ys[6, h] = P(t.matmul(T["p%d" % (4 + h)][:, 0:64], T.wr[:, i, :], T.y6[:, 256 * h + i:256 * h + 256:4], i == 0, i == 3))
+
+    wait("v", ys[5])
+    a = V(v.tensor_tensor_scan(T.scv[:], T.p3[:, 0:128], T.dv[:], -2097152.0, A.max, A.add))
+    wait("v", ys[6, 0])
+    V(v.tensor_tensor_scan(T.scz[:, 0:64], T.p4[:, 0:64], T.dz[:], -2097152.0, A.max, A.add))
+    wait("v", a)
+    V(v.tensor_tensor(T.best[:], T.top[:], T.scv[:, 3::4], A.max))
+    wait("v", ys[6, 1])
+    a = V(v.tensor_tensor_scan(T.scz[:, 64:128], T.p5[:, 0:64], T.dz[:], -2097152.0, A.max, A.add))
+    wait("v", a)
+    a = V(v.tensor_tensor(T.keyi[:], T.best[:], T.scz[:, 3::4], A.max))
+    wait("v", a)
+    a = V(v.tensor_scalar(T.leni[:], T.keyi[:], 16, None, A.arith_shift_right))
+    b = V(v.tensor_scalar(T.idi[:], T.keyi[:], 65535, None, A.bitwise_and))
+    wait("v", a)
+    a = V(v.tensor_scalar(T.yl[:], T.leni[:], 32, None, A.add))
+    wait("v", b)
+    b = V(v.tensor_copy(T.yi[:], T.idi[:]))
+    wait("y", a)
+    done("dyl", sy.dma_start(T.ylen[:], T.yl[:]), 16)
+    wait("s", b)
+    done("dyi", s.dma_start(T.yid[:], T.yi[:]), 16)
+    for name in SEMAPHORES:
+        wait("g", (name, total[name]))

@@ -4,25 +4,25 @@ from concourse.mybir import AluOpType as A, ActivationFunctionType as F
 N = 8
 SCRATCH = {"rl": ("dram", [8, 128, 2], "int32"), "idl": ("dram", [8, 128, 64], "bfloat16"),
            "kraw": ("sbuf", [128, 32, 16], "int32"), "kb": ("sbuf", [128, 8, 64], "bfloat16"),
-           "wr": ("sbuf", [128, 4, 128], "bfloat16"), "wi": ("sbuf", [128, 8, 128], "bfloat16")}
-for _d, _names in (("bfloat16", "win4096 idwin4096 pw384 pf16 bs8 idp384 wlb32 halob8 idhi128 idlo128 iom128 ioa128 blk128 "
-                                "shift128 last128 z512 em592 xa256 xb256"),
-                   ("int32", "wl32 halo32 wa32 wb32 wd32 we32 wf32 wg32 wh32 wj32 wq32 tidr128 ta128 tz128 tl128 pgi1 iop1 ri1 "
-                             "wsi1 keyi32 leni32 idi32"),
-                   ("float32", "lp24 pg1 iof16 rr1 ws1 rm16 eq8 dd4 da4 db4 ca1 cb1 lowr1 ea1 eb1 bc1 bk6 "
-                               "zer32 dk128 dz64 dy192 dv128 sca64 scb64 scy192 scv128 scz128 top32 best32 yl32 yi32"),
-                   ("uint16", "lone2 ltwo2 lpre24 lc32 lq32")):
+           "wk": ("sbuf", [128, 4, 128], "bfloat16")}
+for _d, _names in (("bfloat16", "wr136 wi136 win4096 idwin4096 pw512 pf16 bs16 idp512 wlb32 idr64 idhi64 idlo64 iom128 blk128 "
+                                "shift128 halob8 z128 em592 xs512 dy320"),
+                   ("int32", "wl32 halo32 wa32 wb32 wh32 tidr64 tz64 iop2 ti8 keyi32 leni32 idi32"),
+                   ("float32", "lp32 tf4 eq4 rk4 dd4 da4 ca1 cb1 low1 ea1 eb1 bc1 one2 bk6 wq32 wg32 dk192 sc128 scy320 scz128 "
+                               "yl32 yi32"),
+                   ("uint16", "ltwo4 lpre32 lc32")):
     for _n in _names.split():
         _b = _n.rstrip("0123456789")
         SCRATCH[_b] = ("sbuf", [128, int(_n[len(_b):])], _d)
 for _k in range(1, 7):
-    if _k > 2:
+    if _k > 1:
         SCRATCH["l%d" % _k] = ("sbuf", [128, 32], "uint16")
     SCRATCH["y%d" % _k] = ("sbuf", [128, 512], "bfloat16")
-for _k in range(6):
+for _k in range(5):
     SCRATCH["p%d" % _k] = ("psum", [128, 512], "float32")
-SEMAPHORES = ["cv", "cs", "ct", "cg", "dl", "dr", "dt", "dhi", "dlo", "drr", "didw", "dyl", "dyi"] + \
-             [a + b for a in ("r", "id", "x", "p", "n", "k") for b in ("_in", "_out")] + ["dk%d" % k for k in range(4)]
+SEMAPHORES = ["cv", "cs", "ct", "cg", "dl", "dr", "dt", "dz", "dhi", "dlo", "drr", "didw", "out"] + \
+             [a + "_in" for a in ("r", "id", "x", "p", "k")] + ["dk%d" % k for k in range(4)] + ["dy"]
+OPT = {"order": "xpi", "fill": "dma", "two": 1, "z": "s", "gap": 8, "early": 0}
 
 
 def rank_program(g, core, T, topo):
@@ -30,17 +30,17 @@ def rank_program(g, core, T, topo):
     if me is None:
         return
     q = {"v": g.vector, "s": g.scalar, "t": g.tensor, "g": g, "y": g.sync}
-    total, seen = {}, {k: {} for k in q}
+    total, seen = {name: 0 for name in SEMAPHORES}, {k: {} for k in q}
 
     def wait(k, *toks):
         for tok in toks:
-            if tok is not None and seen[k].get(tok[0], 0) < tok[1]:
+            if seen[k].get(tok[0], 0) < tok[1]:
                 q[k].wait_ge(T.sem[tok[0]], tok[1])
                 seen[k][tok[0]] = tok[1]
 
     def done(sem, inst, n=1):
         inst.then_inc(T.sem[sem], n)
-        total[sem] = total.get(sem, 0) + n
+        total[sem] += n
         return (sem, total[sem])
 
     def V(inst): return done("cv", inst)
@@ -48,12 +48,12 @@ def rank_program(g, core, T, topo):
     def P(inst): return done("ct", inst)
     def G(inst): return done("cg", inst)
     v, s, t, sy = g.vector, g.scalar, g.tensor, g.sync
-    H, NB = N // 2, 48
+    H, BIG = N // 2, 1048576.0
     peers = [T.cores[(me + d) % N] for d in range(1, N)]
     pos = [2 * (j % H) + j // H for j in range(N)]
     at, partner = me % H, T.cores[(me + H) % N]
     near = [T.cores[me - at + (at + d) % H] for d in range(1, H)]
-    wb0, pb0 = 512 * pos[me], NB * pos[me]
+    wb0 = 512 * pos[me]
 
     def dst(c):
         a = topo.addr(c)
@@ -66,13 +66,18 @@ def rank_program(g, core, T, topo):
         ne = bin(mask).count("1")
         g.remote_dma_fused([RemoteDMATransfer(dst_ids=[dst(c) for c in to], dma_engine_mask=mask,
                                               remote_sem=T.sem[name + "_in"], srcs=[src], dsts=[src for c in to])],
-                           local_sem=T.sem[name + "_out"])
-        total[name + "_out"] = ne
-        total[name + "_in"] = ne * len(to)
-        return (name + "_in", ne * len(to))
+                           local_sem=T.sem["out"])
+        total["out"] += ne
+        total[name + "_in"] += ne * len(to)
 
+    def landed(name): return (name + "_in", total[name + "_in"])
+
+    def weights(buf, n, i):
+        return buf[:, n - 1 - i:n + 127 - i]
+
+    tidr, idr, tz, idlo, idhi = [b[0:64, :] for b in (T.tidr, T.idr, T.tz, T.idlo, T.idhi)]
     r_own = done("dr", sy.dma_start(T.rl[me], T.lett[:, 0:32]), 16)
-    tid_ld = done("dt", s.dma_start(T.tidr[0:32, :], T.tid[:]), 16)
+    tid_ld = done("dt", s.dma_start(tidr, T.tid[:]), 16)
     kid_ld = []
     for j in range(4):
         a, gl = j // 2, j % 2
@@ -80,272 +85,260 @@ def rank_program(g, core, T, topo):
                                                              T.kid[gl::2, 4096 * a:4096 * a + 4096]), 16))
     lett_ld = done("dl", sy.dma_start(T.wl[:], T.lett[:]), 16)
 
-    ip = G(g.iota(T.iop[:], [[0, 1]], 0, 1))
+    ip = G(g.iota(T.iop[:], [[0, 2]], 0, 1))
     io = G(g.iota(T.iom[:], [[16, 8], [0, 16]], 0, 0, allow_small_or_imprecise_dtypes=True))
-    iof = G(g.iota(T.iof[:], [[1, 16]], 0, 0, allow_small_or_imprecise_dtypes=True))
-    bs = G(g.iota(T.bs[:], [[512, 8]], 256, 0, allow_small_or_imprecise_dtypes=True))
     idz = V(v.memset(T.idwin[:, 0:512], 0.0))
-    hz = V(v.memset(T.halo[:], 0))
-    V(v.memset(T.pw[:, pb0 + 32:pb0 + NB], 0.0))
     wait("v", ip)
-    V(v.tensor_scalar(T.pgi[:], T.iop[:], 112, None, A.bitwise_and))
-    k0 = V(v.tensor_scalar(T.ri[:], T.iop[:], 15, None, A.bitwise_and))
-    V(v.memset(T.eq[:], 1.0))
-    wait("v", k0)
-    kp = V(v.tensor_copy(T.pg[:], T.pgi[:]))
-    k1 = V(v.tensor_copy(T.rr[:], T.ri[:]))
-    k2 = V(v.tensor_scalar(T.wsi[:], T.ri[:], 2, None, A.arith_shift_right))
-    wait("v", io, kp)
-    bl = V(v.tensor_scalar(T.blk[:], T.iom[:], T.pg[:, 0:1], None, A.is_equal))
-    wait("v", k1, iof)
-    rm = V(v.tensor_scalar(T.rm[:], T.iof[:], T.rr[:, 0:1], None, A.is_equal))
+    k1 = V(v.tensor_scalar(T.ti[:, 4:6], T.iop[:], 14, None, A.bitwise_and))
+    for i, bits in enumerate((112, 15, 12, 3)):
+        k0 = V(v.tensor_scalar(T.ti[:, i:i + 1], T.iop[:, 0:1], bits, None, A.bitwise_and))
+    wait("v", k1)
+    V(v.tensor_scalar(T.one[:], T.ti[:, 4:6], 14 - 2 * me, 256, A.is_equal, A.add))
+    pg, rr, r12, r3 = [T.tf[:, i:i + 1] for i in range(4)]
 
-    wait("v", tid_ld)
-    V(v.tensor_scalar(T.ta[0:32, :], T.tidr[0:32, :], 65280, None, A.bitwise_and))
-    a3 = V(v.tensor_scalar(T.tz[0:32, :], T.tidr[0:32, :], 0, -524288, A.is_equal, A.mult))
-    a4 = V(v.tensor_scalar(T.tl[0:32, :], T.tidr[0:32, :], 255, None, A.bitwise_and))
+    wait("v", tid_ld, k0)
+    V(v.tensor_copy(idr, tidr))
+    a3 = V(v.tensor_scalar(tz, tidr, 0, -524288, A.is_equal, A.mult))
+    V(v.tensor_copy(T.tf[:], T.ti[:, 0:4]))
     wait("v", a3)
-    hi = V(v.tensor_tensor(T.idhi[0:32, :], T.ta[0:32, :], T.tz[0:32, :], A.add))
-    wait("v", a4)
-    lo = V(v.tensor_copy(T.idlo[0:32, :], T.tl[0:32, :]))
-    wait("y", hi)
-    hi_st = done("dhi", sy.dma_start(T.idl[me, 0:64, :], T.idhi[0:32, :]), 16)
+    lo = V(v.tensor_tensor(idlo, tidr, idr, A.subtract))
+    hi = V(v.tensor_tensor(idhi, idr, tz, A.add))
     wait("y", lo)
-    lo_st = done("dlo", sy.dma_start(T.idl[me, 64:128, :], T.idlo[0:32, :]), 16)
+    lo_st = done("dlo", sy.dma_start(T.idl[me, 64:128, :], idlo), 16)
+    wait("y", hi)
+    hi_st = done("dhi", sy.dma_start(T.idl[me, 0:64, :], idhi), 16)
+    if OPT["fill"] == "dma":
+        for n in (3072, 3584):
+            last = done("dz", sy.dma_start(T.idwin[:, n:n + 512], T.idwin[:, 0:512]), 16)
 
     wait("g", r_own)
-    r_in = send(T.rl[me], "r", [T.cores[(me - 1) % N]])
-    io4 = G(g.iota(T.ioa[:], [[16, 8], [0, 4], [1, 4]], 0, 0, allow_small_or_imprecise_dtypes=True))
-    wait("g", hi_st, lo_st)
-    id_in = send(T.idl[me], "id", peers)
+    send(T.rl[me], "r", [T.cores[(me - 1) % N]])
 
-    wait("s", idz)
-    S(s.activation(T.zer[:], T.idwin[:, 0:32], F.Copy))
-    for n in (512, 1024, 2048):
-        idz = S(s.activation(T.idwin[:, n:2 * n], T.idwin[:, 0:n], F.Copy))
-        wait("s", idz)
+    def send_ids(where):
+        if OPT["order"] == where:
+            wait("g", hi_st, lo_st)
+            send(T.idl[me], "id", peers)
+    send_ids("ixp")
+
+    tk = {}
+
+    def constants():
+        wait("v", io)
+        tk["eq"] = V(v.tensor_scalar(T.eq[:], T.iom[:, 0:64:16], 1 / 4, r12, A.mult, A.is_equal))
+        tk["bl"] = V(v.tensor_scalar(T.blk[:], T.iom[:], pg, None, A.is_equal))
+        eu = V(v.tensor_scalar(T.rk[:], T.iom[:, 0:64:16], 1 / 16, r3, A.mult, A.is_equal))
+        V(v.memset(T.wr[:], 0.0))
+        V(v.memset(T.wi[:], 0.0))
+        wait("v", eu)
+        for i in range(4):
+            tk["wk"] = V(v.tensor_scalar(T.wk[:, i, :], T.blk[:], T.rk[:, i:i + 1], None, A.mult))
+        V(v.tensor_tensor(T.dd[:, 0:3], T.eq[:, 0:3], T.eq[:, 1:4], A.subtract))
+        V(v.tensor_scalar(T.low[:], rr, 8.0, BIG, A.is_lt, A.mult))
+        tk["c"] = V(v.tensor_scalar(T.bc[:], rr, 2.0, 4096.0, A.is_equal, A.mult))
 
     for j in range(4):
         a, gl = j // 2, j % 2
         wait("v", kid_ld[j])
-        kc = V(v.tensor_scalar(T.kb[:, :, 32 * a + 16 * gl:32 * a + 16 * gl + 16],
-                               T.kraw[:, 16 * gl + 8 * a:16 * gl + 8 * a + 8, :], 256, None, A.subtract))
+        kc = [V(v.tensor_scalar(T.kb[:, m:n, 32 * a + 16 * gl:32 * a + 16 * gl + 16],
+                                T.kraw[:, 16 * gl + 8 * a + m:16 * gl + 8 * a + n, :], 256, None, A.subtract))
+              for m, n in ([(0, 8)] if j < 3 else [(0, 4), (4, 8)])]
         if j == 1:
-            k3 = V(v.tensor_scalar(T.bc[:], T.rr[:], 2.0, 65536.0, A.is_equal, A.mult))
-            wait("v", k2)
-            k4 = V(v.tensor_copy(T.ws[:], T.wsi[:]))
-    wait("v", kc)
+            tk["hz"] = V(v.memset(T.halo[:], 0))
     for m in (1, 0, 2, 3, 4, 5, 6, 7):
+        wait("v", kc[m // 4])
         ev = V(v.transpose(T.win[:, wb0 + m:wb0 + 512:8], T.kb[:, m, :]))
         if m == 1:
             root = ev
         if m == 6:
             wait("v", root)
-            l1 = V(v.tensor_scalar(T.lone[:, 0:1], T.win[:, wb0 + 1:wb0 + 2], 256, None, A.add))
+            l1 = V(v.tensor_scalar(T.ltwo[:, 0::2], T.one[:], T.win[:, wb0 + 1:wb0 + 2], None, A.add))
+    own, both = T.win[:, wb0:wb0 + 512], T.win[:, 1024 * at:1024 * at + 1024]
     wait("g", ev)
-    x_in = send(T.win[:, wb0:wb0 + 512], "x", [partner])
+    send(own, "x", [partner])
+    send_ids("xip")
 
-    wait("v", ev, l1)
-    g1 = V(v.tensor_copy(T.pf[:], T.win[:, wb0:wb0 + 512].indirect(T.lone[:, 0:1])))
-    V(v.tensor_copy(T.pw[:, pb0 + 34:pb0 + 35], T.win[:, wb0 + 1:wb0 + 2]))
-    wait("v", g1)
-    l2 = V(v.tensor_scalar(T.ltwo[:], T.pf[:, 2 * me:2 * me + 2], 256, None, A.add))
-    V(v.tensor_copy(T.pw[:, pb0 + 32:pb0 + 34], T.pf[:, 2 * me:2 * me + 2]))
-    wait("v", l2)
-    p3 = V(v.tensor_copy(T.pw[:, pb0:pb0 + 32], T.win[:, wb0:wb0 + 512].indirect(T.ltwo[:])))
-    wait("v", k4, lett_ld)
+    wait("v", lett_ld)
     wb = V(v.tensor_copy(T.wlb[:], T.wl[:]))
-    wait("g", p3)
-    p_in = send(T.pw[:, pb0:pb0 + NB], "p", [partner])
-    wait("g", bl)
-    G(g.affine_select(T.shift[:], T.blk[:], [[1, 128]], A.is_equal, 0.0, 1, -1))
-    sh = G(g.affine_select(T.last[:], T.blk[:], [[1, 128]], A.is_equal, 0.0, -15, -1))
-    wait("g", p_in)
-    n_in = send(T.pw[:, 2 * NB * at:2 * NB * at + 2 * NB], "n", near)
-    wait("g", x_in)
-    k_in = send(T.win[:, 1024 * at:1024 * at + 1024], "k", near)
-    for i in range(8):
-        wi = G(g.affine_select(T.wi[:, i, :], T.blk[:], [[0, 16], [1, 8]], A.is_equal, 0.0, -i, 0))
-    wait("y", r_in, hz)
-    rr_ld = done("drr", sy.dma_start(T.halo[0:128:16, :], T.rl[(me + 1) % N]), 16)
-
-    wait("s", wb, rm)
-    for r in range(16):
-        zs = S(s.activation(T.z[:, r::16], T.wlb[:], F.Copy, scale=T.rm[:, r:r + 1]))
-    c1 = V(v.tensor_scalar(T.eq[:, 0:4], T.iof[:, 0:4], T.ws[:, 0:1], None, A.is_equal))
+    wait("v", ev, l1)
+    g1 = V(v.tensor_copy(T.pf[:], own.indirect(T.ltwo[:, 0:1])))
     V(v.tensor_scalar(T.wa[:], T.wl[:], 6, None, A.bitwise_and))
     c2 = V(v.tensor_scalar(T.wb[:], T.wl[:], 3, None, A.arith_shift_right))
-    wait("v", c1)
-    c3 = V(v.tensor_tensor(T.dd[:], T.eq[:, 0:4], T.eq[:, 1:5], A.subtract))
-    low = V(v.tensor_scalar(T.lowr[:], T.ws[:], 2.0, None, A.is_lt))
-    c5 = V(v.tensor_scalar(T.wd[:], T.wl[:], 1, None, A.bitwise_and))
-    wait("v", c2)
-    c2 = V(v.tensor_tensor(T.wq[:], T.wa[:], T.wb[:], A.add))
+    wait("v", g1)
+    l2 = V(v.tensor_scalar(T.ltwo[:, 1::2], T.pf[:, 2 * me:2 * me + 2], 256, None, A.add))
+    c6 = V(v.tensor_scalar(T.wg[:], T.wl[:], 32, None, A.mult))
+    V(v.tensor_scalar(T.lc[:], T.wl[:], 33, None, A.mult))
+    wait("v", l2)
+    p3 = V(v.tensor_copy(T.pw[:, 64 * me:64 * me + 64], own.indirect(T.ltwo[:])))
+    wait("g", p3)
+    send(T.pw[:, 64 * me:64 * me + 64], "p", peers)
+    send_ids("xpi")
+    wait("g", landed("x"))
+    send(both, "k", near)
+    constants()
+    wait("g", tk["bl"])
+    sh = G(g.affine_select(T.shift[:], T.blk[:], [[1, 128]], A.is_equal, 0.0, 1, -1))
+    bs = G(g.iota(T.bs[:], [[512, 2], [1024, 4], [0, 2]], 256, 0, allow_small_or_imprecise_dtypes=True))
+    dyz = G(g.iota(T.dy[:], [[0, 320]], 0, 0, allow_small_or_imprecise_dtypes=True))
+    wait("y", landed("r"), tk["hz"])
+    rr_ld = done("drr", sy.dma_start(T.halo[15:128:16, :], T.rl[(me + 1) % N]), 16)
+
+    fill = [idz]
+    for n in (512, 1024):
+        wait("s", fill[-1])
+        fill.append(S(s.activation(T.idwin[:, n:2 * n], T.idwin[:, 0:n], F.Copy)))
+    fill.append(S(s.activation(T.idwin[:, 2048:3072], T.idwin[:, 0:1024], F.Copy)))
+    if OPT["fill"] == "s":
+        last = S(s.activation(T.idwin[:, 3072:4096], T.idwin[:, 0:1024], F.Copy))
+
+    if OPT["z"] == "s":
+        wait("s", wb, tk["eq"])
+    else:
+        wait("v", tk["eq"])
+    for u in range(4):
+        if OPT["z"] == "s":
+            zs = S(s.activation(T.z[:, u::4], T.wlb[:], F.Copy, scale=T.eq[:, u:u + 1]))
+        else:
+            zs = V(v.tensor_scalar(T.z[:, u::4], T.wl[:], T.eq[:, u:u + 1], None, A.mult))
+    wait("t", zs, tk["wk"])
+    for i in range(4):
+        el = P(t.matmul(T.p2[:, i::4], T.wk[:, i, :], T.z[:], True, True))
+    wq = V(v.tensor_tensor(T.wq[:], T.wa[:], T.wb[:], A.add))
+    wait("v", c6)
+    c6 = V(v.tensor_tensor(T.wh[:, 0:31], T.wg[:, 0:31], T.wl[:, 1:32], A.add))
+    wait("v", el)
+    V(v.tensor_scalar(T.em[:, 512:591], T.p2[:, 1:80], rr, None, A.is_equal))
+    V(v.tensor_scalar(T.em[:, 32:512], T.p2[:, 32:512], rr, None, A.is_equal))
+    wait("v", c6)
+    lq = V(v.tensor_copy(T.l2[:, 0:31], T.wh[:, 0:31]))
     wait("v", rr_ld)
     hb = V(v.tensor_copy(T.halob[:], T.halo[:, 0:8]))
-    wait("v", c5)
-    c5 = V(v.tensor_scalar(T.we[:], T.wd[:], 16, None, A.mult))
-    wait("v", c2)
-    c7 = V(v.tensor_scalar(T.wf[:], T.wq[:], NB, None, A.mult))
-    wait("v", c5)
-    V(v.tensor_tensor(T.wg[:, 0:31], T.we[:, 0:31], T.wl[:, 1:32], A.add))
-    wait("v", c7)
-    c7 = V(v.tensor_tensor(T.wj[:], T.wf[:], T.wl[:], A.add))
-    wait("t", wb, hb, bl, sh)
-    P(t.matmul(T.p3[:, 0:1], T.shift[:], T.wlb[:, 0:1], True, False))
-    cn = P(t.matmul(T.p3[:, 0:1], T.last[:], T.halob[:, 0:1], False, True))
-    P(t.matmul(T.p5[:, 0:5], T.blk[:], T.halob[:, 0:5], True, True))
-    wait("t", zs)
-    el = P(t.matmul(T.p4[:], T.blk[:], T.z[:], True, True))
-    wait("v", io4)
-    for i in range(4):
-        V(v.tensor_scalar(T.wr[:, i, :], T.ioa[:], float(-i), T.pg[:, 0:1], A.add, A.is_equal))
-    wait("v", c7)
-    V(v.tensor_copy(T.lc[:], T.wj[:]))
-    wait("v", cn)
-    c6 = V(v.tensor_scalar(T.wg[:, 31:32], T.we[:, 31:32], T.p3[:, 0:1], None, A.add))
-    wait("v", el)
-    em = V(v.tensor_scalar(T.em[:, 512:591], T.p4[:, 1:80], T.rr[:, 0:1], None, A.is_equal))
-    wait("v", c6)
-    c6 = V(v.tensor_tensor(T.wh[:], T.wf[:], T.wg[:], A.add))
-    V(v.tensor_scalar(T.em[:, 0:512], T.p4[:], T.rr[:, 0:1], None, A.is_equal))
-    wait("v", em, c6)
-    lq = V(v.tensor_copy(T.lq[:], T.wh[:]))
-    em = V(v.tensor_scalar(T.em[:, 527:592:16], T.p5[:, 0:5], T.rr[:, 0:1], None, A.is_equal))
+    wait("t", hb)
+    ex = P(t.matmul(T.p4[:, 0:5], T.blk[:], T.halob[:, 0:5], True, True))
+    wait("t", sh)
+    ext = P(t.matmul(T.p3[:, 0:1], T.shift[:], T.wlb[:, 0:1], True, True))
 
-    wait("s", c3, low, k3, iof)
-    S(s.activation(T.da[:], T.dd[:], F.Identity, scale=16384.0))
-    c4 = S(s.activation(T.ca[:], T.dd[:, 3:4], F.Identity, bias=-7936.0, scale=16384.0))
-    S(s.activation(T.db[:], T.dd[:], F.Identity, scale=1048576.0))
-    S(s.activation(T.cb[:], T.dd[:, 3:4], F.Identity, bias=-2097152.0, scale=1048576.0))
-    S(s.activation(T.ea[:], T.lowr[:], F.Identity, bias=-1048576.0, scale=2097152.0))
-    c8 = S(s.activation(T.eb[:], T.lowr[:], F.Identity, bias=-2097152.0, scale=-1048576.0))
-    S(s.activation(T.bk[:], T.iof[:, 1:7], F.Copy, scale=T.bc[:, 0:1]))
-    wait("s", c4)
+    def id_loads(k, blocks):
+        wait(k, landed("id"), hi_st, lo_st, fill[3], last)
+        for b in blocks:
+            j = pos.index(b)
+            done("didw", q[k].dma_start(T.idwin[0:128:16, 512 * b:512 * b + 512], T.idl[j, 0:64, :]), 16)
+            done("didw", q[k].dma_start(T.idwin[1:128:16, 512 * b:512 * b + 512], T.idl[j, 64:128, :]), 16)
+    id_loads("y", range(0, 4 if OPT["two"] else 8))
+
+    wait("s", tk["c"])
+    S(s.activation(T.da[:, 0:3], T.dd[:, 0:3], F.Identity, scale=BIG))
+    S(s.activation(T.ca[:], T.eq[:, 3:4], F.Identity, bias=-7936.0 - BIG, scale=BIG))
+    S(s.activation(T.cb[:], T.eq[:, 3:4], F.Identity, bias=-3 * BIG, scale=BIG))
+    S(s.activation(T.ea[:], T.low[:], F.Identity, bias=-BIG, scale=2.0))
+    c8 = S(s.activation(T.eb[:], T.low[:], F.Identity, bias=-2 * BIG, scale=-1.0))
+    wr = S(s.activation(T.wr[:, 3:131:4], T.blk[:, ::4], F.Copy))
+    wi = S(s.activation(T.wi[:, 7:135:8], T.blk[:, ::8], F.Copy))
+    S(s.activation(T.bk[:], T.iom[:, 16:112:16], F.Copy, scale=T.bc[:, 0:1]))
+    wait("s", c8, wq)
     for w in range(3):
-        c9 = S(s.activation(T.dk[:, w::4], T.zer[:], F.Identity, bias=T.da[:, w:w + 1]))
-
-    wait("y", id_in, hi_st, lo_st, idz)
-    for j in range(N):
-        b = 512 * pos[j]
-        done("didw", sy.dma_start(T.idwin[0:128:16, b:b + 512], T.idl[j, 0:64, :]), 16)
-        done("didw", sy.dma_start(T.idwin[1:128:16, b:b + 512], T.idl[j, 64:128, :]), 16)
+        S(s.activation(T.dk[:, w::4], T.iom[:, 0:48], F.Identity, bias=T.da[:, w:w + 1], scale=0.0))
+    dk = S(s.activation(T.dk[:, 3:128:4], T.wq[:], F.Identity, bias=T.ca[:, 0:1], scale=512.0))
+    S(s.activation(T.dk[:, 131::4], T.iom[:, 0:16], F.Identity, bias=T.cb[:, 0:1], scale=0.0))
+    if OPT["two"]:
+        id_loads("s", range(4, 8))
     idw = ("didw", total["didw"])
 
-    wait("s", c8)
-    for w in range(4):
-        S(s.activation(T.dz[:, w::4], T.zer[:, 0:16], F.Identity, bias=T.db[:, w:w + 1] if w < 3 else T.cb[:, 0:1]))
-    for d, n in ((T.dy, 3), (T.dv, 2)):
-        for w in range(2 * n):
-            if w in (n - 1, 2 * n - 1):
-                cy = S(s.activation(d[:, w::2 * n], T.zer[:], F.Identity, bias=(T.ea if w == n - 1 else T.eb)[:, 0:1]))
-            else:
-                cy = S(s.activation(d[:, w::2 * n], T.zer[:], F.Copy))
-    X = [T.xa, T.xb]
-    SC = [T.sca, T.scb]
+    ks, sc, lt, yt, ys, yv, GAP = {}, {}, {}, {}, {}, {}, OPT["gap"]
 
-    def kid_sum(h, tok):
-        wait("t", tok)
+    def sum4(h, src, tok):
+        wait("t", tok, wr)
         for i in range(4):
-            r = P(t.matmul(T["p%d" % h][:, 0:64], T.wr[:, i, :], X[h][:, i::4], i == 0, i == 3))
+            r = P(t.matmul(T["p%d" % h][:, 0:64], weights(T.wr, 4, i), src[:, 256 * h + i:256 * h + 256:4], i == 0, i == 3))
         return r
 
-    yt, ys, lt, sc, xt, ks = {}, {}, {}, {}, {}, {}
-
     def id_sum(k):
-        wait("t", yt[k, 0], yt[k, 1], wi)
-        out = T.p2[:, k - 1:192:3] if k < 4 else T.p3[:, k - 4:128:2]
+        wait("t", yt[k], yv.get(k, wi), wi)
         for i in range(8):
-            ys[k] = P(t.matmul(out, T.wi[:, i, :], T["y%d" % k][:, i::8], i == 0, i == 7))
+            ys[k] = P(t.matmul(T.p4[:, k - 1:320:5], weights(T.wi, 8, i), T["y%d" % k][:, i::8], i == 0, i == 7))
 
-    sums = {(3, 1): [1], (4, 1): [2, 3], (5, 1): [4], (6, 0): [5]}
+    sums = {5: 1, 6: 2, 7: 3}
 
-    def scan(k, h):
-        wait("v", ks[h], dcon, c9)
-        sc[h] = V(v.tensor_tensor_scan(SC[h][:], T["p%d" % h][:, 0:64], T.dk[:, 64 * h:64 * h + 64], -8192.0, A.max, A.add))
-
-    def node_list(k, h):
-        wait("v", sc[h])
-        lt[h] = V(v.tensor_scalar(T["l%d" % k][:, 16 * h:16 * h + 16], SC[h][:, 3::4], 8192.0, None, A.add))
-
-    def gathers(k, h):
-        off = T["l%d" % k][:, 16 * h:16 * h + 16]
-        y, bias = T["y%d" % k][:, 256 * h:256 * h + 256], T.bk[:, k - 1:k]
-        if k < 6:
-            wait("v", lt[h], x_in, k_in, ev)
-            xt[h] = V(v.tensor_tensor(X[h][:], T.win[:].indirect(off), T.em[:, 16 * (k + 16 * h):16 * (k + 16 * h) + 256],
-                                      A.mult))
-            ks[h] = kid_sum(h, xt[h])
-        if k < 6 or h == 0:
-            wait("s", lt[h], idw)
-            yt[k, h] = S(s.activation(y, T.idwin[:].indirect(off), F.Identity, bias=bias))
+    def gather(n):
+        k, h = 2 + n // 2, n % 2
+        if n == 0:
+            wait("v", lq, p3, landed("p"), bs)
+            V(v.tensor_tensor(T.lp[:, 0::2], T.pw[:, 15:481:31], T.bs[:], A.add))
+            tk["lp"] = V(v.tensor_tensor(T.lp[:, 1::2], T.pw[:, 0::33], T.bs[:], A.add))
+        elif n == 1:
+            wait("v", tk["ends"])
         else:
-            wait("v", lt[h], idw)
-            yt[k, h] = V(v.tensor_scalar(y, T.idwin[:].indirect(off), bias, None, A.add))
-        for a in sums.get((k, h), []):
-            id_sum(a)
-
-    for h in range(2):
-        wait("v", em, lq, p3, p_in, n_in)
-        xt[h] = V(v.tensor_tensor(X[h][:], T.pw[:].indirect(T.lq[:, 16 * h:16 * h + 16]),
-                                  T.em[:, 16 * (2 + 16 * h):16 * (2 + 16 * h) + 256], A.mult))
-        ks[h] = kid_sum(h, xt[h])
-        if h == 0:
-            wait("v", bs)
-            for i in range(3):
-                b = V(v.tensor_tensor(T.lp[:, i::3], T.pw[:, 32 + i::NB], T.bs[:], A.add))
-            wait("v", c4)
-            dcon = V(v.tensor_scalar(T.dk[:, 3::4], T.wq[:], 512.0, T.ca[:, 0:1], A.mult, A.add))
-            wait("v", b)
+            wait("v", lt[n - 2], landed("x"), landed("k"))
+        xt = V(v.tensor_tensor(T.xs[:, 256 * h:256 * h + 256],
+                               (T.pw[:, 16:512] if k == 2 else T.win[:]).indirect(T["l%d" % k][:, 16 * h:16 * h + 16]),
+                               T.em[:, 16 * k + 256 * h:16 * k + 256 * h + 256], A.mult))
+        ks[n] = sum4(h, T.xs, xt)
+        if n in sums:
+            id_sum(sums[n])
+        if n == 0:
+            wait("v", ext, ex, tk["lp"])
+            V(v.tensor_scalar(T.l2[:, 31:32], T.halo[:, 0:1], T.p3[:, 0:1], T.wg[:, 31:32], A.add, A.add))
+            tk["ends"] = V(v.tensor_scalar(T.em[:, 527:592:16], T.p4[:, 0:5], rr, None, A.is_equal))
             lp = V(v.tensor_copy(T.lpre[:], T.lp[:]))
-    wait("s", lp, idw, cy)
-    idp = S(s.activation(T.idp[:], T.idwin[:].indirect(T.lpre[:]), F.Copy))
-    wait("s", idp)
-    for h in range(2):
-        yt[1, h] = S(s.activation(T.y1[:, 256 * h:256 * h + 256], T.idp[:, 32:384].indirect(T.lc[:, 16 * h:16 * h + 16]),
-                                  F.Identity, bias=T.bk[:, 0:1]))
-    for h in range(2):
-        yt[2, h] = S(s.activation(T.y2[:, 256 * h:256 * h + 256], T.idp[:].indirect(T.lq[:, 16 * h:16 * h + 16]),
-                                  F.Identity, bias=T.bk[:, 1:2]))
+            wait("s", lp, idw)
+            idp = S(s.activation(T.idp[:], T.idwin[:].indirect(T.lpre[:]), F.Copy))
+            wait("s", dyz)
+            S(s.activation(T.dy[:, 4::10], T.iom[:, 0:32], F.Identity, bias=T.ea[:, 0:1], scale=0.0))
+            tk["dy"] = S(s.activation(T.dy[:, 9::10], T.iom[:, 0:32], F.Identity, bias=T.eb[:, 0:1], scale=0.0))
+            wait("s", idp)
+            yt[1] = S(s.activation(T.y1[:], T.idp[:].indirect(T.lc[:]), F.Identity, bias=T.bk[:, 0:1]))
+            yt[2] = S(s.activation(T.y2[:], T.idp[:, 16:512].indirect(T.l2[:]), F.Identity, bias=T.bk[:, 1:2]))
 
-    for k in range(3, 7):
-        scan(k, 0)
-        if k == 6:
-            wait("v", ys[3], cy)
-            b = V(v.tensor_tensor_scan(T.scy[:], T.p2[:, 0:192], T.dy[:], -2097152.0, A.max, A.add))
-        scan(k, 1)
-        for h in range(2):
-            node_list(k, h)
-        if k == 6:
-            wait("v", b)
-            V(v.tensor_scalar(T.top[:], T.scy[:, 5::6], -2097152.0, None, A.max))
-        for h in range(2):
-            gathers(k, h)
-    for h in range(2):
-        wait("t", yt[6, h])
-        for i in range(4):
-            ys[6, h] = P(t.matmul(T["p%d" % (4 + h)][:, 0:64], T.wr[:, i, :], T.y6[:, 256 * h + i:256 * h + 256:4], i == 0, i == 3))
+    def scan(n):
+        k, h = 2 + n // 2, n % 2
+        if h and k > 2 and GAP:
+            wait("v", idw)
+            yv[k] = V(v.tensor_scalar(T["y%d" % k][:, 512 - 16 * GAP:512], T.idwin[:].indirect(T["l%d" % k][:, 32 - GAP:32]),
+                                      T.bk[:, k - 1:k], None, A.add))
+        wait("v", ks[n], dk)
+        sc[n] = V(v.tensor_tensor_scan(T.sc[:, 64 * h:64 * h + 64], T["p%d" % h][:, 0:64], T.dk[:, 64 * h:64 * h + 64], -8192.0,
+                                       A.max, A.add))
 
-    wait("v", ys[5])
-    a = V(v.tensor_tensor_scan(T.scv[:], T.p3[:, 0:128], T.dv[:], -2097152.0, A.max, A.add))
-    wait("v", ys[6, 0])
-    V(v.tensor_tensor_scan(T.scz[:, 0:64], T.p4[:, 0:64], T.dz[:], -2097152.0, A.max, A.add))
+    def node_list(n):
+        k, h = 3 + n // 2, n % 2
+        off, y = T["l%d" % k][:, 16 * h:16 * h + 16], T["y%d" % k][:, 256 * h:256 * h + 256]
+        wait("v", sc[n])
+        lt[n] = V(v.tensor_scalar(off, T.sc[:, 64 * h + 3:64 * h + 64:4], 8192.0, None, A.add))
+        if n < 7:
+            if h:
+                off, y = T["l%d" % k][:, 16:32 - GAP], T["y%d" % k][:, 256:512 - 16 * GAP]
+            wait("s", lt[n])
+            yt[k] = yt[k, h] = S(s.activation(y, T.idwin[:].indirect(off), F.Identity, bias=T.bk[:, k - 1:k]))
+        else:
+            wait("v", lt[n], idw)
+            yt[k, h] = V(v.tensor_scalar(y, T.idwin[:].indirect(off), T.bk[:, k - 1:k], None, A.add))
+
+    for n in range(0, 8, 2):
+        for f in (gather, scan, node_list):
+            f(n)
+            f(n + 1)
+    id_sum(4)
+    id_sum(5)
+    for h in range(2):
+        ys[6, h] = sum4(h, T.y6, yt[6, h])
+
+    wait("v", ys[5], tk["dy"])
+    V(v.tensor_tensor_scan(T.scy[:], T.p4[:, 0:320], T.dy[:], -2 * BIG, A.max, A.add))
+    for h in range(2):
+        wait("v", ys[6, h])
+        a = V(v.tensor_tensor_scan(T.scz[:, 64 * h:64 * h + 64], T["p%d" % h][:, 0:64], T.dk[:, 128:192], -2 * BIG,
+                                   A.max, A.add))
     wait("v", a)
-    V(v.tensor_tensor(T.best[:], T.top[:], T.scv[:, 3::4], A.max))
-    wait("v", ys[6, 1])
-    a = V(v.tensor_tensor_scan(T.scz[:, 64:128], T.p5[:, 0:64], T.dz[:], -2097152.0, A.max, A.add))
-    wait("v", a)
-    a = V(v.tensor_tensor(T.keyi[:], T.best[:], T.scz[:, 3::4], A.max))
+    a = V(v.tensor_tensor(T.keyi[:], T.scy[:, 9::10], T.scz[:, 3::4], A.max))
     wait("v", a)
     a = V(v.tensor_scalar(T.leni[:], T.keyi[:], 16, None, A.arith_shift_right))
     b = V(v.tensor_scalar(T.idi[:], T.keyi[:], 65535, None, A.bitwise_and))
     wait("v", a)
-    a = V(v.tensor_scalar(T.yl[:], T.leni[:], 32, None, A.add))
+    a = V(v.tensor_scalar(T.yl[:], T.leni[:], 32, 0, A.add, A.max))
     wait("v", b)
     b = V(v.tensor_copy(T.yi[:], T.idi[:]))
     wait("y", a)
-    done("dyl", sy.dma_start(T.ylen[:], T.yl[:]), 16)
+    done("dy", sy.dma_start(T.ylen[:], T.yl[:]), 16)
     wait("s", b)
-    done("dyi", s.dma_start(T.yid[:], T.yi[:]), 16)
+    done("dy", s.dma_start(T.yid[:], T.yi[:]), 16)
     for name in SEMAPHORES:
         wait("g", (name, total[name]))

@@ -1,16 +1,16 @@
 from concourse.bass import DstId, RemoteDMATransfer
-from concourse.mybir import AluOpType as A, ActivationFunctionType as F
+from concourse.mybir import AluOpType as A, ActivationFunctionType as F, AxisListType as X
 
 N = 8
-SCRATCH = {"rl": ("dram", [8, 128, 2], "int32"), "idl": ("dram", [8, 128, 64], "bfloat16"),
+SCRATCH = {"rl": ("dram", [128, 8], "int32"), "lf": ("dram", [128, 32], "int32"), "idl": ("dram", [8, 128, 64], "bfloat16"),
            "kraw": ("sbuf", [128, 32, 16], "int32"), "kb": ("sbuf", [128, 8, 64], "bfloat16"),
            "wk": ("sbuf", [128, 4, 128], "bfloat16")}
-for _d, _names in (("bfloat16", "wr136 wi136 win4096 idwin4096 pw512 pf16 bs16 idp512 wlb32 idr64 idhi64 idlo64 iom128 blk128 "
-                                "shift128 halob8 z128 em592 xs512 dy320"),
-                   ("int32", "wl32 halo32 wa32 wb32 wh32 tidr64 tz64 iop2 ti8 keyi32 leni32 idi32"),
-                   ("float32", "lp32 tf4 eq4 rk4 dd4 da4 ca1 cb1 low1 ea1 eb1 bc1 one2 bk6 wq32 wg32 dk192 sc128 scy320 scz128 "
+for _d, _names in (("bfloat16", "wr136 wi136 win4096 idwin4096 pw512 idp272 bs16 wlb32 idr64 idhi64 idlo64 iom128 blk128 "
+                                "halob8 z128 em592 xs512 dy320"),
+                   ("int32", "wl32 wn2 halo8 wa32 wb32 wh32 tidr64 tz64 iop1 ti8 keyi32 leni32 idi32"),
+                   ("float32", "lp16 rq1 rb1 rsum1 tf4 eq4 rk4 dd4 da4 ca1 cb1 low1 ea1 eb1 bc1 wz1 inn1 one2 rim2 bk6 wq32 wg32 dk192 sc128 scy320 scz128 "
                                "yl32 yi32"),
-                   ("uint16", "ltwo4 lpre32 lc32")):
+                   ("uint16", "lone2 ltwo16 lpre16 ls32 lc32")):
     for _n in _names.split():
         _b = _n.rstrip("0123456789")
         SCRATCH[_b] = ("sbuf", [128, int(_n[len(_b):])], _d)
@@ -20,9 +20,9 @@ for _k in range(1, 7):
     SCRATCH["y%d" % _k] = ("sbuf", [128, 512], "bfloat16")
 for _k in range(5):
     SCRATCH["p%d" % _k] = ("psum", [128, 512], "float32")
-SEMAPHORES = ["cv", "cs", "ct", "cg", "dl", "dr", "dt", "dz", "dhi", "dlo", "drr", "didw", "out"] + \
+SEMAPHORES = ["cv", "cs", "ct", "cg", "dl", "dr", "dt", "dz", "do", "dlo", "didw", "out", "df", "de"] + \
              [a + "_in" for a in ("r", "id", "x", "p", "k")] + ["dk%d" % k for k in range(4)] + ["dy"]
-OPT = {"order": "xpi", "fill": "dma", "two": 1, "z": "s", "gap": 8, "early": 0}
+OPT = {"order": "xpi", "p1": 7, "dma": 2, "v": 0, "wks": 4, "gap": {3: 6, 4: 6, 5: 8, 6: 10}, "la": 1}
 
 
 def rank_program(g, core, T, topo):
@@ -59,13 +59,14 @@ def rank_program(g, core, T, topo):
         a = topo.addr(c)
         return DstId(rid=a[0], pnc=a[1])
 
-    def send(src, name, to):
+    def send(src, name, to, out=None):
+        out = src if out is None else out
         mask = topo.mask(core, to[0])
         for c in to:
             mask = mask & topo.mask(core, c)
         ne = bin(mask).count("1")
         g.remote_dma_fused([RemoteDMATransfer(dst_ids=[dst(c) for c in to], dma_engine_mask=mask,
-                                              remote_sem=T.sem[name + "_in"], srcs=[src], dsts=[src for c in to])],
+                                              remote_sem=T.sem[name + "_in"], srcs=[src], dsts=[out for c in to])],
                            local_sem=T.sem["out"])
         total["out"] += ne
         total[name + "_in"] += ne * len(to)
@@ -76,171 +77,191 @@ def rank_program(g, core, T, topo):
         return buf[:, n - 1 - i:n + 127 - i]
 
     tidr, idr, tz, idlo, idhi = [b[0:64, :] for b in (T.tidr, T.idr, T.tz, T.idlo, T.idhi)]
-    r_own = done("dr", sy.dma_start(T.rl[me], T.lett[:, 0:32]), 16)
+    r_own = done("dr", sy.dma_start(T.rl[:], T.lett[:, 0:128]), 16)
     tid_ld = done("dt", s.dma_start(tidr, T.tid[:]), 16)
     kid_ld = []
     for j in range(4):
         a, gl = j // 2, j % 2
         kid_ld.append(done("dk%d" % j, (sy, s)[gl].dma_start(T.kraw[:, 16 * gl + 8 * a:16 * gl + 8 * a + 8, :],
                                                              T.kid[gl::2, 4096 * a:4096 * a + 4096]), 16))
+
+    def convert(j):
+        a, gl = j // 2, j % 2
+        wait("v", kid_ld[j])
+        return [V(v.tensor_scalar(T.kb[:, m:n, 32 * a + 16 * gl:32 * a + 16 * gl + 16],
+                                  T.kraw[:, 16 * gl + 8 * a + m:16 * gl + 8 * a + n, :], 256, None, A.subtract))
+                for m, n in ([(0, 8)] if j < 3 else [(0, 4), (4, 8)])]
     lett_ld = done("dl", sy.dma_start(T.wl[:], T.lett[:]), 16)
+    lf = done("df", sy.dma_start(T.lf[:], T.lett[:]), 16)
 
-    ip = G(g.iota(T.iop[:], [[0, 2]], 0, 1))
+    ip = G(g.iota(T.iop[:], [[0, 1]], 0, 1))
     io = G(g.iota(T.iom[:], [[16, 8], [0, 16]], 0, 0, allow_small_or_imprecise_dtypes=True))
-    idz = V(v.memset(T.idwin[:, 0:512], 0.0))
+    idb = [T.idwin[:, 512 * b:512 * b + 512] for b in [(pos[me] + d) % N for d in range(N)]]
+    idz = V(v.memset(idb[0], 0.0))
     wait("v", ip)
-    k1 = V(v.tensor_scalar(T.ti[:, 4:6], T.iop[:], 14, None, A.bitwise_and))
     for i, bits in enumerate((112, 15, 12, 3)):
-        k0 = V(v.tensor_scalar(T.ti[:, i:i + 1], T.iop[:, 0:1], bits, None, A.bitwise_and))
-    wait("v", k1)
-    V(v.tensor_scalar(T.one[:], T.ti[:, 4:6], 14 - 2 * me, 256, A.is_equal, A.add))
+        k0 = V(v.tensor_scalar(T.ti[:, i:i + 1], T.iop[:], bits, None, A.bitwise_and))
+    V(v.memset(T.one[:], 256.0))
+    V(v.memset(T.wn[96:128, :], 0))
+    wait("v", k0)
+    k0 = V(v.tensor_copy(T.tf[:], T.ti[:, 0:4]))
     pg, rr, r12, r3 = [T.tf[:, i:i + 1] for i in range(4)]
+    wait("s", idz)
+    zero = S(s.activation(idb[1], idb[0], F.Copy))
+    wait("s", zero)
+    for b in idb[2:4]:
+        S(s.activation(b, idb[1], F.Copy))
+    wait("y", idz)
+    last = idz
+    for b in idb[8 - OPT["dma"]:8]:
+        last = done("dz", sy.dma_start(b, idb[0]), 16)
 
-    wait("v", tid_ld, k0)
+    wait("v", tid_ld)
     V(v.tensor_copy(idr, tidr))
     a3 = V(v.tensor_scalar(tz, tidr, 0, -524288, A.is_equal, A.mult))
-    V(v.tensor_copy(T.tf[:], T.ti[:, 0:4]))
+    wait("v", io, k0)
+    V(v.tensor_scalar(T.blk[:], T.iom[:], pg, None, A.is_equal))
+    V(v.tensor_scalar(T.rk[:], T.iom[:, 0:64:16], 1 / 16, r3, A.mult, A.is_equal))
     wait("v", a3)
     lo = V(v.tensor_tensor(idlo, tidr, idr, A.subtract))
     hi = V(v.tensor_tensor(idhi, idr, tz, A.add))
     wait("y", lo)
-    lo_st = done("dlo", sy.dma_start(T.idl[me, 64:128, :], idlo), 16)
+    done("dlo", sy.dma_start(T.idl[me, 64:128, :], idlo), 16)
     wait("y", hi)
-    hi_st = done("dhi", sy.dma_start(T.idl[me, 0:64, :], idhi), 16)
-    if OPT["fill"] == "dma":
-        for n in (3072, 3584):
-            last = done("dz", sy.dma_start(T.idwin[:, n:n + 512], T.idwin[:, 0:512]), 16)
+    hi_st = done("dlo", sy.dma_start(T.idl[me, 0:64, :], idhi), 16)
+    wait("y", lf)
+    ext = done("de", sy.dma_start(T.wn[0:127, :], T.lf[1:128, 0:2]), 16)
+    wait("y", zero)
 
     wait("g", r_own)
-    send(T.rl[me], "r", [T.cores[(me - 1) % N]])
+    send(T.rl[:], "r", [T.cores[(me - 1) % N]], T.halo[:])
 
     def send_ids(where):
         if OPT["order"] == where:
-            wait("g", hi_st, lo_st)
+            wait("g", hi_st)
             send(T.idl[me], "id", peers)
     send_ids("ixp")
 
     tk = {}
 
     def constants():
-        wait("v", io)
-        tk["eq"] = V(v.tensor_scalar(T.eq[:], T.iom[:, 0:64:16], 1 / 4, r12, A.mult, A.is_equal))
-        tk["bl"] = V(v.tensor_scalar(T.blk[:], T.iom[:], pg, None, A.is_equal))
-        eu = V(v.tensor_scalar(T.rk[:], T.iom[:, 0:64:16], 1 / 16, r3, A.mult, A.is_equal))
-        V(v.memset(T.wr[:], 0.0))
-        V(v.memset(T.wi[:], 0.0))
-        wait("v", eu)
-        for i in range(4):
+        for i in range(4 - OPT["wks"]):
             tk["wk"] = V(v.tensor_scalar(T.wk[:, i, :], T.blk[:], T.rk[:, i:i + 1], None, A.mult))
+        V(v.tensor_scalar(T.rim[:], T.iom[:, 0:32:16], 15 / 16, rr, A.mult, A.is_equal))
+        tk["wr"] = V(v.memset(T.wr[:], 0.0))
         V(v.tensor_tensor(T.dd[:, 0:3], T.eq[:, 0:3], T.eq[:, 1:4], A.subtract))
-        V(v.tensor_scalar(T.low[:], rr, 8.0, BIG, A.is_lt, A.mult))
-        tk["c"] = V(v.tensor_scalar(T.bc[:], rr, 2.0, 4096.0, A.is_equal, A.mult))
+        tk["c"] = V(v.tensor_scalar(T.low[:], rr, 8.0, BIG, A.is_lt, A.mult))
 
+    tk["wk"] = lo
+    wait("s", lo)
+    for i in range(4 - OPT["wks"], 4):
+        S(s.activation(T.wk[:, i, :], T.blk[:], F.Copy, scale=T.rk[:, i:i + 1]))
     for j in range(4):
-        a, gl = j // 2, j % 2
-        wait("v", kid_ld[j])
-        kc = [V(v.tensor_scalar(T.kb[:, m:n, 32 * a + 16 * gl:32 * a + 16 * gl + 16],
-                                T.kraw[:, 16 * gl + 8 * a + m:16 * gl + 8 * a + n, :], 256, None, A.subtract))
-              for m, n in ([(0, 8)] if j < 3 else [(0, 4), (4, 8)])]
-        if j == 1:
-            tk["hz"] = V(v.memset(T.halo[:], 0))
+        kc = convert(j)
     for m in (1, 0, 2, 3, 4, 5, 6, 7):
         wait("v", kc[m // 4])
         ev = V(v.transpose(T.win[:, wb0 + m:wb0 + 512:8], T.kb[:, m, :]))
         if m == 1:
             root = ev
-        if m == 6:
+        if m == 7:
             wait("v", root)
-            l1 = V(v.tensor_scalar(T.ltwo[:, 0::2], T.one[:], T.win[:, wb0 + 1:wb0 + 2], None, A.add))
+            l1 = V(v.tensor_scalar(T.lone[:], T.one[:], T.win[:, wb0 + 1:wb0 + 2], None, A.add))
     own, both = T.win[:, wb0:wb0 + 512], T.win[:, 1024 * at:1024 * at + 1024]
     wait("g", ev)
-    send(own, "x", [partner])
+    eng = [e for e in topo.engines(core, partner) if e in topo.engines(core, near[0])]
+    g.remote_dma_fused([RemoteDMATransfer(dst_ids=[dst(c)], dma_engine_mask=sum(1 << e for e in eng[i::2]),
+                                          remote_sem=T.sem[name + "_in"], srcs=[own], dsts=[own])
+                        for i, (name, c) in enumerate((("x", partner), ("k", near[0])))], local_sem=T.sem["out"])
+    for name, n in (("out", len(eng)), ("x_in", len(eng) // 2), ("k_in", len(eng) // 2)):
+        total[name] += n
     send_ids("xip")
 
+    pb0, two = 64 * me, T.ltwo[:, 2 * me:2 * me + 2]
+    V(v.tensor_scalar(T.eq[:], T.iom[:, 0:64:16], 1 / 4, r12, A.mult, A.is_equal))
     wait("v", lett_ld)
     wb = V(v.tensor_copy(T.wlb[:], T.wl[:]))
     wait("v", ev, l1)
-    g1 = V(v.tensor_copy(T.pf[:], own.indirect(T.ltwo[:, 0:1])))
+    g1 = V(v.tensor_scalar(T.ltwo[:], own.indirect(T.lone[:, 0:1]), 256, None, A.add))
+    V(v.tensor_copy(T.pw[:, pb0 + 1:pb0 + 64:2], own.indirect(T.lone[:])))
+    wait("v", g1)
+    p3 = V(v.tensor_copy(T.pw[:, pb0:pb0 + 64:2], own.indirect(two)))
+    wait("g", p3)
+    send(T.pw[:, pb0:pb0 + 64], "p", peers[:OPT["p1"]])
+    send_ids("xpi")
+    if OPT["p1"] < 7:
+        send(T.pw[:, pb0:pb0 + 64], "p", peers[OPT["p1"]:])
+    constants()
+    c6 = V(v.tensor_scalar(T.wg[:], T.wl[:], 16, None, A.mult))
     V(v.tensor_scalar(T.wa[:], T.wl[:], 6, None, A.bitwise_and))
     c2 = V(v.tensor_scalar(T.wb[:], T.wl[:], 3, None, A.arith_shift_right))
-    wait("v", g1)
-    l2 = V(v.tensor_scalar(T.ltwo[:, 1::2], T.pf[:, 2 * me:2 * me + 2], 256, None, A.add))
-    c6 = V(v.tensor_scalar(T.wg[:], T.wl[:], 32, None, A.mult))
-    V(v.tensor_scalar(T.lc[:], T.wl[:], 33, None, A.mult))
-    wait("v", l2)
-    p3 = V(v.tensor_copy(T.pw[:, 64 * me:64 * me + 64], own.indirect(T.ltwo[:])))
-    wait("g", p3)
-    send(T.pw[:, 64 * me:64 * me + 64], "p", peers)
-    send_ids("xpi")
     wait("g", landed("x"))
-    send(both, "k", near)
-    constants()
-    wait("g", tk["bl"])
-    sh = G(g.affine_select(T.shift[:], T.blk[:], [[1, 128]], A.is_equal, 0.0, 1, -1))
+    send(both, "k", near[1:])
+    wb1 = 512 * pos[(me + H) % N]
+    send(T.win[:, wb1:wb1 + 512], "k", near[:1])
+    gz = idz
+    for b in idb[5:5 + OPT["v"]]:
+        gz = G(g.iota(b, [[0, 512]], 0, 0, allow_small_or_imprecise_dtypes=True))
     bs = G(g.iota(T.bs[:], [[512, 2], [1024, 4], [0, 2]], 256, 0, allow_small_or_imprecise_dtypes=True))
+    wiz = G(g.iota(T.wi[:], [[0, 136]], 0, 0, allow_small_or_imprecise_dtypes=True))
     dyz = G(g.iota(T.dy[:], [[0, 320]], 0, 0, allow_small_or_imprecise_dtypes=True))
-    wait("y", landed("r"), tk["hz"])
-    rr_ld = done("drr", sy.dma_start(T.halo[15:128:16, :], T.rl[(me + 1) % N]), 16)
 
-    fill = [idz]
-    for n in (512, 1024):
-        wait("s", fill[-1])
-        fill.append(S(s.activation(T.idwin[:, n:2 * n], T.idwin[:, 0:n], F.Copy)))
-    fill.append(S(s.activation(T.idwin[:, 2048:3072], T.idwin[:, 0:1024], F.Copy)))
-    if OPT["fill"] == "s":
-        last = S(s.activation(T.idwin[:, 3072:4096], T.idwin[:, 0:1024], F.Copy))
-
-    if OPT["z"] == "s":
-        wait("s", wb, tk["eq"])
-    else:
-        wait("v", tk["eq"])
+    wait("s", wb)
     for u in range(4):
-        if OPT["z"] == "s":
-            zs = S(s.activation(T.z[:, u::4], T.wlb[:], F.Copy, scale=T.eq[:, u:u + 1]))
-        else:
-            zs = V(v.tensor_scalar(T.z[:, u::4], T.wl[:], T.eq[:, u:u + 1], None, A.mult))
+        zs = S(s.activation(T.z[:, u::4], T.wlb[:], F.Copy, scale=T.eq[:, u:u + 1]))
+    wait("s", tk["wr"])
+    inn = S(s.activation(T.inn[:], T.rim[:, 1:2], F.Identity, bias=1.0, scale=-1.0))
+    bc = S(s.activation(T.bc[:], T.rim[:, 1:2], F.Identity, scale=4096.0))
+    wr = S(s.activation(T.wr[:, 3:131:4], T.blk[:, ::4], F.Copy))
+    fill = S(s.activation(idb[4], idb[1], F.Copy))
     wait("t", zs, tk["wk"])
     for i in range(4):
         el = P(t.matmul(T.p2[:, i::4], T.wk[:, i, :], T.z[:], True, True))
-    wq = V(v.tensor_tensor(T.wq[:], T.wa[:], T.wb[:], A.add))
     wait("v", c6)
     c6 = V(v.tensor_tensor(T.wh[:, 0:31], T.wg[:, 0:31], T.wl[:, 1:32], A.add))
-    wait("v", el)
-    V(v.tensor_scalar(T.em[:, 512:591], T.p2[:, 1:80], rr, None, A.is_equal))
-    V(v.tensor_scalar(T.em[:, 32:512], T.p2[:, 32:512], rr, None, A.is_equal))
-    wait("v", c6)
-    lq = V(v.tensor_copy(T.l2[:, 0:31], T.wh[:, 0:31]))
-    wait("v", rr_ld)
-    hb = V(v.tensor_copy(T.halob[:], T.halo[:, 0:8]))
+    V(v.tensor_scalar(T.ti[:, 4:5], T.iop[:], 14, None, A.bitwise_and))
+    wait("v", c2)
+    wq = V(v.tensor_tensor(T.wq[:], T.wa[:], T.wb[:], A.add))
+    wait("v", landed("r"))
+    hb = V(v.tensor_scalar(T.halob[:], T.halo[:], T.rim[:, 0:1], None, A.mult))
     wait("t", hb)
     ex = P(t.matmul(T.p4[:, 0:5], T.blk[:], T.halob[:, 0:5], True, True))
-    wait("t", sh)
-    ext = P(t.matmul(T.p3[:, 0:1], T.shift[:], T.wlb[:, 0:1], True, True))
+    wait("v", ext, inn)
+    c6 = V(v.tensor_scalar(T.wz[:], T.wn[:, 0:1], T.inn[:, 0:1], T.wg[:, 31:32], A.mult, A.add))
+    wait("v", el)
+    V(v.tensor_scalar(T.em[:, 512:591], T.p2[:, 1:80], rr, None, A.is_equal))
+    wait("v", ex, c6)
+    c6 = V(v.tensor_scalar(T.wh[:, 31:32], T.p4[:, 0:1], T.rim[:, 1:2], T.wz[:, 0:1], A.mult, A.add))
+    V(v.tensor_scalar(T.em[:, 32:288], T.p2[:, 32:288], rr, None, A.is_equal))
+    wait("v", c6)
+    lq = V(v.tensor_scalar(T.l2[:], T.wh[:], 2, None, A.mult))
+    V(v.tensor_scalar(T.em[:, 527:592:16], T.p4[:, 0:5], rr, None, A.is_equal))
+    emb = V(v.tensor_scalar(T.em[:, 288:512], T.p2[:, 288:512], rr, None, A.is_equal))
 
-    def id_loads(k, blocks):
-        wait(k, landed("id"), hi_st, lo_st, fill[3], last)
-        for b in blocks:
-            j = pos.index(b)
-            done("didw", q[k].dma_start(T.idwin[0:128:16, 512 * b:512 * b + 512], T.idl[j, 0:64, :]), 16)
-            done("didw", q[k].dma_start(T.idwin[1:128:16, 512 * b:512 * b + 512], T.idl[j, 64:128, :]), 16)
-    id_loads("y", range(0, 4 if OPT["two"] else 8))
+    def id_loads(k, ranks, parts):
+        for j in ranks:
+            for r in parts:
+                done("didw", q[k].dma_start(T.idwin[r:128:16, 512 * pos[j]:512 * pos[j] + 512], T.idl[j, 64 * r:64 * r + 64, :]), 16)
 
-    wait("s", tk["c"])
+    wait("s", tk["c"], bc)
     S(s.activation(T.da[:, 0:3], T.dd[:, 0:3], F.Identity, scale=BIG))
     S(s.activation(T.ca[:], T.eq[:, 3:4], F.Identity, bias=-7936.0 - BIG, scale=BIG))
     S(s.activation(T.cb[:], T.eq[:, 3:4], F.Identity, bias=-3 * BIG, scale=BIG))
     S(s.activation(T.ea[:], T.low[:], F.Identity, bias=-BIG, scale=2.0))
+    S(s.activation(T.rq[:], T.low[:], F.Identity, bias=-1536.0, scale=3584.0 / BIG))
     c8 = S(s.activation(T.eb[:], T.low[:], F.Identity, bias=-2 * BIG, scale=-1.0))
-    wr = S(s.activation(T.wr[:, 3:131:4], T.blk[:, ::4], F.Copy))
-    wi = S(s.activation(T.wi[:, 7:135:8], T.blk[:, ::8], F.Copy))
     S(s.activation(T.bk[:], T.iom[:, 16:112:16], F.Copy, scale=T.bc[:, 0:1]))
     wait("s", c8, wq)
     for w in range(3):
         S(s.activation(T.dk[:, w::4], T.iom[:, 0:48], F.Identity, bias=T.da[:, w:w + 1], scale=0.0))
     dk = S(s.activation(T.dk[:, 3:128:4], T.wq[:], F.Identity, bias=T.ca[:, 0:1], scale=512.0))
     S(s.activation(T.dk[:, 131::4], T.iom[:, 0:16], F.Identity, bias=T.cb[:, 0:1], scale=0.0))
-    if OPT["two"]:
-        id_loads("s", range(4, 8))
+    for b in idb[5 + OPT["v"]:8 - OPT["dma"]]:
+        fill = S(s.activation(b, idb[1], F.Copy))
+    wait("y", hi_st, last)
+    id_loads("y", [me], (0, 1))
+    for r, k in enumerate("ys"):
+        wait(k, fill, last, gz, landed("id"))
+        id_loads(k, [(me + d) % N for d in range(1, N)], (r,))
     idw = ("didw", total["didw"])
 
     ks, sc, lt, yt, ys, yv, GAP = {}, {}, {}, {}, {}, {}, OPT["gap"]
@@ -252,74 +273,92 @@ def rank_program(g, core, T, topo):
         return r
 
     def id_sum(k):
-        wait("t", yt[k], yv.get(k, wi), wi)
+        wait("t", yt[k], yv.get(k, yt[k]))
         for i in range(8):
             ys[k] = P(t.matmul(T.p4[:, k - 1:320:5], weights(T.wi, 8, i), T["y%d" % k][:, i::8], i == 0, i == 7))
 
-    sums = {5: 1, 6: 2, 7: 3}
+    def ids(e, k, a, b):
+        out, src, bias = T["y%d" % k][:, 16 * a:16 * b], T.idwin[:].indirect(T["l%d" % k][:, a:b]), T.bk[:, k - 1:k]
+        wait(e, idw)
+        return S(s.activation(out, src, F.Identity, bias=bias)) if e == "s" else V(v.tensor_scalar(out, src, bias, None, A.add))
+
+    sums = {5: 3, 6: 2, 7: 4}
 
     def gather(n):
         k, h = 2 + n // 2, n % 2
         if n == 0:
-            wait("v", lq, p3, landed("p"), bs)
-            V(v.tensor_tensor(T.lp[:, 0::2], T.pw[:, 15:481:31], T.bs[:], A.add))
-            tk["lp"] = V(v.tensor_tensor(T.lp[:, 1::2], T.pw[:, 0::33], T.bs[:], A.add))
-        elif n == 1:
-            wait("v", tk["ends"])
-        else:
-            wait("v", lt[n - 2], landed("x"), landed("k"))
+            wait("v", landed("x"), emb, landed("p"))
+        elif n > 1:
+            wait("v", lt[n - 2], landed("k"))
         xt = V(v.tensor_tensor(T.xs[:, 256 * h:256 * h + 256],
-                               (T.pw[:, 16:512] if k == 2 else T.win[:]).indirect(T["l%d" % k][:, 16 * h:16 * h + 16]),
+                               (T.pw if k == 2 else T.win)[:].indirect(T["l%d" % k][:, 16 * h:16 * h + 16]),
                                T.em[:, 16 * k + 256 * h:16 * k + 256 * h + 256], A.mult))
         ks[n] = sum4(h, T.xs, xt)
         if n in sums:
             id_sum(sums[n])
-        if n == 0:
-            wait("v", ext, ex, tk["lp"])
-            V(v.tensor_scalar(T.l2[:, 31:32], T.halo[:, 0:1], T.p3[:, 0:1], T.wg[:, 31:32], A.add, A.add))
-            tk["ends"] = V(v.tensor_scalar(T.em[:, 527:592:16], T.p4[:, 0:5], rr, None, A.is_equal))
-            lp = V(v.tensor_copy(T.lpre[:], T.lp[:]))
-            wait("s", lp, idw)
-            idp = S(s.activation(T.idp[:], T.idwin[:].indirect(T.lpre[:]), F.Copy))
-            wait("s", dyz)
-            S(s.activation(T.dy[:, 4::10], T.iom[:, 0:32], F.Identity, bias=T.ea[:, 0:1], scale=0.0))
-            tk["dy"] = S(s.activation(T.dy[:, 9::10], T.iom[:, 0:32], F.Identity, bias=T.eb[:, 0:1], scale=0.0))
-            wait("s", idp)
-            yt[1] = S(s.activation(T.y1[:], T.idp[:].indirect(T.lc[:]), F.Identity, bias=T.bk[:, 0:1]))
-            yt[2] = S(s.activation(T.y2[:], T.idp[:, 16:512].indirect(T.l2[:]), F.Identity, bias=T.bk[:, 1:2]))
+
+        if n == 1:
+            wait("v", bs)
+            tk["lp"] = V(v.tensor_tensor(T.lp[:], T.pw[:, 1::34], T.bs[:], A.add))
 
     def scan(n):
         k, h = 2 + n // 2, n % 2
-        if h and k > 2 and GAP:
-            wait("v", idw)
-            yv[k] = V(v.tensor_scalar(T["y%d" % k][:, 512 - 16 * GAP:512], T.idwin[:].indirect(T["l%d" % k][:, 32 - GAP:32]),
-                                      T.bk[:, k - 1:k], None, A.add))
+        if n == 1:
+            wait("v", tk["lp"])
+            lp = V(v.tensor_copy(T.lpre[:], T.lp[:]))
+            V(v.tensor_copy(T.lc[:], T.wl[:]))
+            V(v.tensor_copy(T.ls[:], T.wh[:]))
+            wait("s", dyz)
+            S(s.activation(T.wi[:, 7:135:8], T.blk[:, ::8], F.Copy))
+            S(s.activation(T.dy[:, 4::10], T.iom[:, 0:32], F.Identity, bias=T.ea[:, 0:1], scale=0.0))
+            tk["dy"] = S(s.activation(T.dy[:, 9::10], T.iom[:, 0:32], F.Identity, bias=T.eb[:, 0:1], scale=0.0))
+            wait("s", lp, idw)
+            tk["id2"] = S(s.activation(T.idp[:, 16:272], T.idwin[:].indirect(T.lpre[:]), F.Copy))
+        if n == 3:
+            tk["r"] = V(v.tensor_reduce(T.rsum[:], T.win[:, 1::512], X.X, A.add))
+            wait("s", tk["id2"])
+            yt[2] = S(s.activation(T.y2[:], T.idp[:, 16:272].indirect(T.ls[:]), F.Identity, bias=T.bk[:, 1:2]))
+        if n == 5:
+            wait("v", tk["r"])
+            yt[1] = V(v.tensor_copy(T.idp[:, 0:16], T.idwin[:].indirect(T.lone[:, 0:1])))
+            wait("s", yt[1])
+            yt[1] = S(s.activation(T.y1[:], T.idp[:, 0:16].indirect(T.lc[:]), F.Identity, bias=T.bk[:, 0:1]))
+        if h and k > 2 and GAP[k]:
+            yv[k] = ids("v", k, 32 - GAP[k], 32)
+        if n == 7:
+            node_list(n - 1)
         wait("v", ks[n], dk)
         sc[n] = V(v.tensor_tensor_scan(T.sc[:, 64 * h:64 * h + 64], T["p%d" % h][:, 0:64], T.dk[:, 64 * h:64 * h + 64], -8192.0,
                                        A.max, A.add))
 
     def node_list(n):
         k, h = 3 + n // 2, n % 2
-        off, y = T["l%d" % k][:, 16 * h:16 * h + 16], T["y%d" % k][:, 256 * h:256 * h + 256]
         wait("v", sc[n])
-        lt[n] = V(v.tensor_scalar(off, T.sc[:, 64 * h + 3:64 * h + 64:4], 8192.0, None, A.add))
-        if n < 7:
-            if h:
-                off, y = T["l%d" % k][:, 16:32 - GAP], T["y%d" % k][:, 256:512 - 16 * GAP]
+        lt[n] = V(v.tensor_scalar(T["l%d" % k][:, 16 * h:16 * h + 16], T.sc[:, 64 * h + 3:64 * h + 64:4], 8192.0, None, A.add))
+        if 16 * h < 32 - GAP[k]:
             wait("s", lt[n])
-            yt[k] = yt[k, h] = S(s.activation(y, T.idwin[:].indirect(off), F.Identity, bias=T.bk[:, k - 1:k]))
-        else:
-            wait("v", lt[n], idw)
-            yt[k, h] = V(v.tensor_scalar(y, T.idwin[:].indirect(off), T.bk[:, k - 1:k], None, A.add))
+            yt[k] = yt[k, h] = ids("s", k, 16 * h, 32 - GAP[k] if h else 16)
 
     for n in range(0, 8, 2):
-        for f in (gather, scan, node_list):
-            f(n)
-            f(n + 1)
-    id_sum(4)
-    id_sum(5)
-    for h in range(2):
-        ys[6, h] = sum4(h, T.y6, yt[6, h])
+        gather(n)
+        gather(n + 1)
+        scan(n)
+        scan(n + 1)
+        if n < 6:
+            node_list(n)
+        if n == 0:
+            V(v.tensor_scalar(T.rb[:], T.ti[:, 4:5], 512.0, T.rq[:, 0:1], A.mult, A.add))
+        if n == 2:
+            wait("v", tk["r"])
+            tk["r"] = V(v.tensor_scalar(T.lone[:, 0:1], T.rsum[:], T.rb[:, 0:1], None, A.add))
+        node_list(n + 1)
+    wait("v", lt[7])
+    yv[6] = ids("v", 6, 32 - GAP[6], 32)
+    for k in (1, 5):
+        id_sum(k)
+    ys[6, 0] = sum4(0, T.y6, yt[6, 0])
+    wait("t", yt[6])
+    ys[6, 1] = sum4(1, T.y6, yv[6])
 
     wait("v", ys[5], tk["dy"])
     V(v.tensor_tensor_scan(T.scy[:], T.p4[:, 0:320], T.dy[:], -2 * BIG, A.max, A.add))

from concourse.bass import DstId, RemoteDMATransfer
from concourse.mybir import AluOpType as A, ActivationFunctionType as F, AxisListType as X

N = 8
SCRATCH = {"rl": ("dram", [128, 8], "int32"), "lf": ("dram", [128, 32], "int32"), "idl": ("dram", [8, 128, 64], "bfloat16"),
           "kraw": ("sbuf", [128, 32, 16], "int32"), "kb": ("sbuf", [128, 8, 64], "bfloat16"),
           "wk": ("sbuf", [128, 4, 128], "bfloat16")}
for _d, _names in (("bfloat16", "wr136 wi136 win4096 idwin4096 pw512 idp272 bs16 wlb32 idr64 idhi64 idlo64 iom128 blk128 "
                                "halob8 z128 em592 xs512 dy320"),
                   ("int32", "wl32 wn2 halo8 wa32 wb32 wh32 tidr64 tz64 iop1 ti8 keyi32 leni32 idi32"),
                   ("float32", "lp16 rq1 rb1 rsum1 tf4 eq4 rk4 dd4 da4 ca1 cb1 low1 ea1 eb1 bc1 wz1 inn1 one2 rim2 bk6 wq32 wg32 dk192 sc128 scy320 scz128 "
                               "yl32 yi32"),
                   ("uint16", "lone2 ltwo16 lpre16 ls32 lc32")):
    for _n in _names.split():
        _b = _n.rstrip("0123456789")
        SCRATCH[_b] = ("sbuf", [128, int(_n[len(_b):])], _d)
for _k in range(1, 7):
    if _k > 1:
        SCRATCH["l%d" % _k] = ("sbuf", [128, 32], "uint16")
    SCRATCH["y%d" % _k] = ("sbuf", [128, 512], "bfloat16")
for _k in range(5):
    SCRATCH["p%d" % _k] = ("psum", [128, 512], "float32")
SEMAPHORES = ["cv", "cs", "ct", "cg", "dl", "dr", "dt", "dz", "do", "dlo", "didw", "out", "df", "de"] + \
             [a + "_in" for a in ("r", "id", "x", "p", "k")] + ["dk%d" % k for k in range(4)] + ["dy"]
OPT = {"order": "xpi", "p1": 7, "dma": 2, "v": 0, "wks": 4, "gap": {3: 6, 4: 6, 5: 8, 6: 10}, "la": 1}


def rank_program(g, core, T, topo):
    me = T.rank_of(core)
    if me is None:
        return
    q = {"v": g.vector, "s": g.scalar, "t": g.tensor, "g": g, "y": g.sync}
    total, seen = {name: 0 for name in SEMAPHORES}, {k: {} for k in q}

    def wait(k, *toks):
        for tok in toks:
            if seen[k].get(tok[0], 0) < tok[1]:
                q[k].wait_ge(T.sem[tok[0]], tok[1])
                seen[k][tok[0]] = tok[1]

    def done(sem, inst, n=1):
        inst.then_inc(T.sem[sem], n)
        total[sem] += n
        return (sem, total[sem])

    def V(inst): return done("cv", inst)
    def S(inst): return done("cs", inst)
    def P(inst): return done("ct", inst)
    def G(inst): return done("cg", inst)
    v, s, t, sy = g.vector, g.scalar, g.tensor, g.sync
    H, BIG = N // 2, 1048576.0
    peers = [T.cores[(me + d) % N] for d in range(1, N)]
    pos = [2 * (j % H) + j // H for j in range(N)]
    at, partner = me % H, T.cores[(me + H) % N]
    near = [T.cores[me - at + (at + d) % H] for d in range(1, H)]
    wb0 = 512 * pos[me]

    def dst(c):
        a = topo.addr(c)
        return DstId(rid=a[0], pnc=a[1])

    def send(src, name, to, out=None):
        out = src if out is None else out
        mask = topo.mask(core, to[0])
        for c in to:
            mask = mask & topo.mask(core, c)
        ne = bin(mask).count("1")
        g.remote_dma_fused([RemoteDMATransfer(dst_ids=[dst(c) for c in to], dma_engine_mask=mask,
                                              remote_sem=T.sem[name + "_in"], srcs=[src], dsts=[out for c in to])],
                           local_sem=T.sem["out"])
        total["out"] += ne
        total[name + "_in"] += ne * len(to)

    def landed(name): return (name + "_in", total[name + "_in"])

    def weights(buf, n, i):
        return buf[:, n - 1 - i:n + 127 - i]

    tidr, idr, tz, idlo, idhi = [b[0:64, :] for b in (T.tidr, T.idr, T.tz, T.idlo, T.idhi)]
    r_own = done("dr", sy.dma_start(T.rl[:], T.lett[:, 0:128]), 16)
    tid_ld = done("dt", s.dma_start(tidr, T.tid[:]), 16)
    kid_ld = []
    for j in range(4):
        a, gl = j // 2, j % 2
        kid_ld.append(done("dk%d" % j, (sy, s)[gl].dma_start(T.kraw[:, 16 * gl + 8 * a:16 * gl + 8 * a + 8, :],
                                                             T.kid[gl::2, 4096 * a:4096 * a + 4096]), 16))

    def convert(j):
        a, gl = j // 2, j % 2
        wait("v", kid_ld[j])
        return [V(v.tensor_scalar(T.kb[:, m:n, 32 * a + 16 * gl:32 * a + 16 * gl + 16],
                                  T.kraw[:, 16 * gl + 8 * a + m:16 * gl + 8 * a + n, :], 256, None, A.subtract))
                for m, n in ([(0, 8)] if j < 3 else [(0, 4), (4, 8)])]
    lett_ld = done("dl", sy.dma_start(T.wl[:], T.lett[:]), 16)
    lf = done("df", sy.dma_start(T.lf[:], T.lett[:]), 16)

    ip = G(g.iota(T.iop[:], [[0, 1]], 0, 1))
    io = G(g.iota(T.iom[:], [[16, 8], [0, 16]], 0, 0, allow_small_or_imprecise_dtypes=True))
    idb = [T.idwin[:, 512 * b:512 * b + 512] for b in [(pos[me] + d) % N for d in range(N)]]
    idz = V(v.memset(idb[0], 0.0))
    wait("v", ip)
    for i, bits in enumerate((112, 15, 12, 3)):
        k0 = V(v.tensor_scalar(T.ti[:, i:i + 1], T.iop[:], bits, None, A.bitwise_and))
    V(v.memset(T.one[:], 256.0))
    V(v.memset(T.wn[96:128, :], 0))
    wait("v", k0)
    k0 = V(v.tensor_copy(T.tf[:], T.ti[:, 0:4]))
    pg, rr, r12, r3 = [T.tf[:, i:i + 1] for i in range(4)]
    wait("s", idz)
    zero = S(s.activation(idb[1], idb[0], F.Copy))
    wait("s", zero)
    for b in idb[2:4]:
        S(s.activation(b, idb[1], F.Copy))
    wait("y", idz)
    last = idz
    for b in idb[8 - OPT["dma"]:8]:
        last = done("dz", sy.dma_start(b, idb[0]), 16)

    wait("v", tid_ld)
    V(v.tensor_copy(idr, tidr))
    a3 = V(v.tensor_scalar(tz, tidr, 0, -524288, A.is_equal, A.mult))
    wait("v", io, k0)
    V(v.tensor_scalar(T.blk[:], T.iom[:], pg, None, A.is_equal))
    V(v.tensor_scalar(T.rk[:], T.iom[:, 0:64:16], 1 / 16, r3, A.mult, A.is_equal))
    wait("v", a3)
    lo = V(v.tensor_tensor(idlo, tidr, idr, A.subtract))
    hi = V(v.tensor_tensor(idhi, idr, tz, A.add))
    wait("y", lo)
    done("dlo", sy.dma_start(T.idl[me, 64:128, :], idlo), 16)
    wait("y", hi)
    hi_st = done("dlo", sy.dma_start(T.idl[me, 0:64, :], idhi), 16)
    wait("y", lf)
    ext = done("de", sy.dma_start(T.wn[0:127, :], T.lf[1:128, 0:2]), 16)
    wait("y", zero)

    wait("g", r_own)
    send(T.rl[:], "r", [T.cores[(me - 1) % N]], T.halo[:])

    def send_ids(where):
        if OPT["order"] == where:
            wait("g", hi_st)
            send(T.idl[me], "id", peers)
    send_ids("ixp")

    tk = {}

    def constants():
        for i in range(4 - OPT["wks"]):
            tk["wk"] = V(v.tensor_scalar(T.wk[:, i, :], T.blk[:], T.rk[:, i:i + 1], None, A.mult))
        V(v.tensor_scalar(T.rim[:], T.iom[:, 0:32:16], 15 / 16, rr, A.mult, A.is_equal))
        tk["wr"] = V(v.memset(T.wr[:], 0.0))
        V(v.tensor_tensor(T.dd[:, 0:3], T.eq[:, 0:3], T.eq[:, 1:4], A.subtract))
        tk["c"] = V(v.tensor_scalar(T.low[:], rr, 8.0, BIG, A.is_lt, A.mult))

    tk["wk"] = lo
    wait("s", lo)
    for i in range(4 - OPT["wks"], 4):
        S(s.activation(T.wk[:, i, :], T.blk[:], F.Copy, scale=T.rk[:, i:i + 1]))
    for j in range(4):
        kc = convert(j)
    for m in (1, 0, 2, 3, 4, 5, 6, 7):
        wait("v", kc[m // 4])
        ev = V(v.transpose(T.win[:, wb0 + m:wb0 + 512:8], T.kb[:, m, :]))
        if m == 1:
            root = ev
        if m == 7:
            wait("v", root)
            l1 = V(v.tensor_scalar(T.lone[:], T.one[:], T.win[:, wb0 + 1:wb0 + 2], None, A.add))
    own, both = T.win[:, wb0:wb0 + 512], T.win[:, 1024 * at:1024 * at + 1024]
    wait("g", ev)
    eng = [e for e in topo.engines(core, partner) if e in topo.engines(core, near[0])]
    g.remote_dma_fused([RemoteDMATransfer(dst_ids=[dst(c)], dma_engine_mask=sum(1 << e for e in eng[i::2]),
                                          remote_sem=T.sem[name + "_in"], srcs=[own], dsts=[own])
                        for i, (name, c) in enumerate((("x", partner), ("k", near[0])))], local_sem=T.sem["out"])
    for name, n in (("out", len(eng)), ("x_in", len(eng) // 2), ("k_in", len(eng) // 2)):
        total[name] += n
    send_ids("xip")

    pb0, two = 64 * me, T.ltwo[:, 2 * me:2 * me + 2]
    V(v.tensor_scalar(T.eq[:], T.iom[:, 0:64:16], 1 / 4, r12, A.mult, A.is_equal))
    wait("v", lett_ld)
    wb = V(v.tensor_copy(T.wlb[:], T.wl[:]))
    wait("v", ev, l1)
    g1 = V(v.tensor_scalar(T.ltwo[:], own.indirect(T.lone[:, 0:1]), 256, None, A.add))
    V(v.tensor_copy(T.pw[:, pb0 + 1:pb0 + 64:2], own.indirect(T.lone[:])))
    wait("v", g1)
    p3 = V(v.tensor_copy(T.pw[:, pb0:pb0 + 64:2], own.indirect(two)))
    wait("g", p3)
    send(T.pw[:, pb0:pb0 + 64], "p", peers[:OPT["p1"]])
    send_ids("xpi")
    if OPT["p1"] < 7:
        send(T.pw[:, pb0:pb0 + 64], "p", peers[OPT["p1"]:])
    constants()
    c6 = V(v.tensor_scalar(T.wg[:], T.wl[:], 16, None, A.mult))
    V(v.tensor_scalar(T.wa[:], T.wl[:], 6, None, A.bitwise_and))
    c2 = V(v.tensor_scalar(T.wb[:], T.wl[:], 3, None, A.arith_shift_right))
    wait("g", landed("x"))
    send(both, "k", near[1:])
    wb1 = 512 * pos[(me + H) % N]
    send(T.win[:, wb1:wb1 + 512], "k", near[:1])
    gz = idz
    for b in idb[5:5 + OPT["v"]]:
        gz = G(g.iota(b, [[0, 512]], 0, 0, allow_small_or_imprecise_dtypes=True))
    bs = G(g.iota(T.bs[:], [[512, 2], [1024, 4], [0, 2]], 256, 0, allow_small_or_imprecise_dtypes=True))
    wiz = G(g.iota(T.wi[:], [[0, 136]], 0, 0, allow_small_or_imprecise_dtypes=True))
    dyz = G(g.iota(T.dy[:], [[0, 320]], 0, 0, allow_small_or_imprecise_dtypes=True))

    wait("s", wb)
    for u in range(4):
        zs = S(s.activation(T.z[:, u::4], T.wlb[:], F.Copy, scale=T.eq[:, u:u + 1]))
    wait("s", tk["wr"])
    inn = S(s.activation(T.inn[:], T.rim[:, 1:2], F.Identity, bias=1.0, scale=-1.0))
    bc = S(s.activation(T.bc[:], T.rim[:, 1:2], F.Identity, scale=4096.0))
    wr = S(s.activation(T.wr[:, 3:131:4], T.blk[:, ::4], F.Copy))
    fill = S(s.activation(idb[4], idb[1], F.Copy))
    wait("t", zs, tk["wk"])
    for i in range(4):
        el = P(t.matmul(T.p2[:, i::4], T.wk[:, i, :], T.z[:], True, True))
    wait("v", c6)
    c6 = V(v.tensor_tensor(T.wh[:, 0:31], T.wg[:, 0:31], T.wl[:, 1:32], A.add))
    V(v.tensor_scalar(T.ti[:, 4:5], T.iop[:], 14, None, A.bitwise_and))
    wait("v", c2)
    wq = V(v.tensor_tensor(T.wq[:], T.wa[:], T.wb[:], A.add))
    wait("v", landed("r"))
    hb = V(v.tensor_scalar(T.halob[:], T.halo[:], T.rim[:, 0:1], None, A.mult))
    wait("t", hb)
    ex = P(t.matmul(T.p4[:, 0:5], T.blk[:], T.halob[:, 0:5], True, True))
    wait("v", ext, inn)
    c6 = V(v.tensor_scalar(T.wz[:], T.wn[:, 0:1], T.inn[:, 0:1], T.wg[:, 31:32], A.mult, A.add))
    wait("v", el)
    V(v.tensor_scalar(T.em[:, 512:591], T.p2[:, 1:80], rr, None, A.is_equal))
    wait("v", ex, c6)
    c6 = V(v.tensor_scalar(T.wh[:, 31:32], T.p4[:, 0:1], T.rim[:, 1:2], T.wz[:, 0:1], A.mult, A.add))
    V(v.tensor_scalar(T.em[:, 32:288], T.p2[:, 32:288], rr, None, A.is_equal))
    wait("v", c6)
    lq = V(v.tensor_scalar(T.l2[:], T.wh[:], 2, None, A.mult))
    V(v.tensor_scalar(T.em[:, 527:592:16], T.p4[:, 0:5], rr, None, A.is_equal))
    emb = V(v.tensor_scalar(T.em[:, 288:512], T.p2[:, 288:512], rr, None, A.is_equal))

    def id_loads(k, ranks, parts):
        for j in ranks:
            for r in parts:
                done("didw", q[k].dma_start(T.idwin[r:128:16, 512 * pos[j]:512 * pos[j] + 512], T.idl[j, 64 * r:64 * r + 64, :]), 16)

    wait("s", tk["c"], bc)
    S(s.activation(T.da[:, 0:3], T.dd[:, 0:3], F.Identity, scale=BIG))
    S(s.activation(T.ca[:], T.eq[:, 3:4], F.Identity, bias=-7936.0 - BIG, scale=BIG))
    S(s.activation(T.cb[:], T.eq[:, 3:4], F.Identity, bias=-3 * BIG, scale=BIG))
    S(s.activation(T.ea[:], T.low[:], F.Identity, bias=-BIG, scale=2.0))
    S(s.activation(T.rq[:], T.low[:], F.Identity, bias=-1536.0, scale=3584.0 / BIG))
    c8 = S(s.activation(T.eb[:], T.low[:], F.Identity, bias=-2 * BIG, scale=-1.0))
    S(s.activation(T.bk[:], T.iom[:, 16:112:16], F.Copy, scale=T.bc[:, 0:1]))
    wait("s", c8, wq)
    for w in range(3):
        S(s.activation(T.dk[:, w::4], T.iom[:, 0:48], F.Identity, bias=T.da[:, w:w + 1], scale=0.0))
    dk = S(s.activation(T.dk[:, 3:128:4], T.wq[:], F.Identity, bias=T.ca[:, 0:1], scale=512.0))
    S(s.activation(T.dk[:, 131::4], T.iom[:, 0:16], F.Identity, bias=T.cb[:, 0:1], scale=0.0))
    for b in idb[5 + OPT["v"]:8 - OPT["dma"]]:
        fill = S(s.activation(b, idb[1], F.Copy))
    wait("y", hi_st, last)
    id_loads("y", [me], (0, 1))
    for r, k in enumerate("ys"):
        wait(k, fill, last, gz, landed("id"))
        id_loads(k, [(me + d) % N for d in range(1, N)], (r,))
    idw = ("didw", total["didw"])

    ks, sc, lt, yt, ys, yv, GAP = {}, {}, {}, {}, {}, {}, OPT["gap"]

    def sum4(h, src, tok):
        wait("t", tok, wr)
        for i in range(4):
            r = P(t.matmul(T["p%d" % h][:, 0:64], weights(T.wr, 4, i), src[:, 256 * h + i:256 * h + 256:4], i == 0, i == 3))
        return r

    def id_sum(k):
        wait("t", yt[k], yv.get(k, yt[k]))
        for i in range(8):
            ys[k] = P(t.matmul(T.p4[:, k - 1:320:5], weights(T.wi, 8, i), T["y%d" % k][:, i::8], i == 0, i == 7))

    def ids(e, k, a, b):
        out, src, bias = T["y%d" % k][:, 16 * a:16 * b], T.idwin[:].indirect(T["l%d" % k][:, a:b]), T.bk[:, k - 1:k]
        wait(e, idw)
        return S(s.activation(out, src, F.Identity, bias=bias)) if e == "s" else V(v.tensor_scalar(out, src, bias, None, A.add))

    sums = {5: 3, 6: 2, 7: 4}

    def gather(n):
        k, h = 2 + n // 2, n % 2
        if n == 0:
            wait("v", landed("x"), emb, landed("p"))
        elif n > 1:
            wait("v", lt[n - 2], landed("k"))
        xt = V(v.tensor_tensor(T.xs[:, 256 * h:256 * h + 256],
                               (T.pw if k == 2 else T.win)[:].indirect(T["l%d" % k][:, 16 * h:16 * h + 16]),
                               T.em[:, 16 * k + 256 * h:16 * k + 256 * h + 256], A.mult))
        ks[n] = sum4(h, T.xs, xt)
        if n in sums:
            id_sum(sums[n])

        if n == 1:
            wait("v", bs)
            tk["lp"] = V(v.tensor_tensor(T.lp[:], T.pw[:, 1::34], T.bs[:], A.add))

    def scan(n):
        k, h = 2 + n // 2, n % 2
        if n == 1:
            wait("v", tk["lp"])
            lp = V(v.tensor_copy(T.lpre[:], T.lp[:]))
            V(v.tensor_copy(T.lc[:], T.wl[:]))
            V(v.tensor_copy(T.ls[:], T.wh[:]))
            wait("s", dyz)
            S(s.activation(T.wi[:, 7:135:8], T.blk[:, ::8], F.Copy))
            S(s.activation(T.dy[:, 4::10], T.iom[:, 0:32], F.Identity, bias=T.ea[:, 0:1], scale=0.0))
            tk["dy"] = S(s.activation(T.dy[:, 9::10], T.iom[:, 0:32], F.Identity, bias=T.eb[:, 0:1], scale=0.0))
            wait("s", lp, idw)
            tk["id2"] = S(s.activation(T.idp[:, 16:272], T.idwin[:].indirect(T.lpre[:]), F.Copy))
        if n == 3:
            tk["r"] = V(v.tensor_reduce(T.rsum[:], T.win[:, 1::512], X.X, A.add))
            wait("s", tk["id2"])
            yt[2] = S(s.activation(T.y2[:], T.idp[:, 16:272].indirect(T.ls[:]), F.Identity, bias=T.bk[:, 1:2]))
        if n == 5:
            wait("v", tk["r"])
            yt[1] = V(v.tensor_copy(T.idp[:, 0:16], T.idwin[:].indirect(T.lone[:, 0:1])))
            wait("s", yt[1])
            yt[1] = S(s.activation(T.y1[:], T.idp[:, 0:16].indirect(T.lc[:]), F.Identity, bias=T.bk[:, 0:1]))
        if h and k > 2 and GAP[k]:
            yv[k] = ids("v", k, 32 - GAP[k], 32)
        if n == 7:
            node_list(n - 1)
        wait("v", ks[n], dk)
        sc[n] = V(v.tensor_tensor_scan(T.sc[:, 64 * h:64 * h + 64], T["p%d" % h][:, 0:64], T.dk[:, 64 * h:64 * h + 64], -8192.0,
                                       A.max, A.add))

    def node_list(n):
        k, h = 3 + n // 2, n % 2
        wait("v", sc[n])
        lt[n] = V(v.tensor_scalar(T["l%d" % k][:, 16 * h:16 * h + 16], T.sc[:, 64 * h + 3:64 * h + 64:4], 8192.0, None, A.add))
        if 16 * h < 32 - GAP[k]:
            wait("s", lt[n])
            yt[k] = yt[k, h] = ids("s", k, 16 * h, 32 - GAP[k] if h else 16)

    for n in range(0, 8, 2):
        gather(n)
        gather(n + 1)
        scan(n)
        scan(n + 1)
        if n < 6:
            node_list(n)
        if n == 0:
            V(v.tensor_scalar(T.rb[:], T.ti[:, 4:5], 512.0, T.rq[:, 0:1], A.mult, A.add))
        if n == 2:
            wait("v", tk["r"])
            tk["r"] = V(v.tensor_scalar(T.lone[:, 0:1], T.rsum[:], T.rb[:, 0:1], None, A.add))
        node_list(n + 1)
    wait("v", lt[7])
    yv[6] = ids("v", 6, 32 - GAP[6], 32)
    for k in (1, 5):
        id_sum(k)
    ys[6, 0] = sum4(0, T.y6, yt[6, 0])
    wait("t", yt[6])
    ys[6, 1] = sum4(1, T.y6, yv[6])

    wait("v", ys[5], tk["dy"])
    V(v.tensor_tensor_scan(T.scy[:], T.p4[:, 0:320], T.dy[:], -2 * BIG, A.max, A.add))
    for h in range(2):
        wait("v", ys[6, h])
        a = V(v.tensor_tensor_scan(T.scz[:, 64 * h:64 * h + 64], T["p%d" % h][:, 0:64], T.dk[:, 128:192], -2 * BIG,
                                   A.max, A.add))
    wait("v", a)
    a = V(v.tensor_tensor(T.keyi[:], T.scy[:, 9::10], T.scz[:, 3::4], A.max))
    wait("v", a)
    a = V(v.tensor_scalar(T.leni[:], T.keyi[:], 16, None, A.arith_shift_right))
    b = V(v.tensor_scalar(T.idi[:], T.keyi[:], 65535, None, A.bitwise_and))
    wait("v", a)
    a = V(v.tensor_scalar(T.yl[:], T.leni[:], 32, 0, A.add, A.max))
    wait("v", b)
    b = V(v.tensor_copy(T.yi[:], T.idi[:]))
    wait("y", a)
    done("dy", sy.dma_start(T.ylen[:], T.yl[:]), 16)
    wait("s", b)
    done("dy", s.dma_start(T.yid[:], T.yi[:]), 16)
    for name in SEMAPHORES:
        wait("g", (name, total[name]))
